import numpy as np, ml_dtypes
CORES = [5,29,101,125,133,157,229,253]
N = 8
import mx_ref
BF = ml_dtypes.bfloat16
def gcols(t, e):
    v = np.concatenate([t.reshape(8, 16, -1, 4), np.zeros((8, 16, 1, 4), BF)], axis=2)
    return np.ascontiguousarray(np.stack([v[g][:, e[g]] for g in range(8)])).reshape(128, -1)
def tile(rs):
    return np.stack(rs, axis=2).reshape(128, -1).astype(BF)
def pick(q, e):
    c = np.concatenate([q[0].reshape(128, -1, 4), np.zeros((128, 1, 4), np.uint8)], axis=1); s = np.concatenate([q[1], np.ones((16, 1), np.uint8)], axis=1)
    return (np.ascontiguousarray(c[:, e].reshape(128, -1)), np.ascontiguousarray(s[:, e]))
def join(*qs):
    return (np.concatenate([q[0] for q in qs], axis=1), np.concatenate([q[1] for q in qs], axis=1))
def put(q, e, v):
    c, s = q[0].reshape(128, -1, 4).copy(), q[1].copy(); c[:, e] = v[0].reshape(128, -1, 4); s[:, e] = v[1]
    return (c.reshape(128, -1), s)
def pk(c, s):
    return (np.ascontiguousarray(c), mx_ref.live(s))
def emit(q):
    return q[0], q[1]
def packed(v, rng):
    q = [mx_ref.quantize(np.ascontiguousarray(v[r])) for r in range(N)]
    return np.stack([a for a, b in q]), np.stack([mx_ref.plane(b, rng) for a, b in q])
def values_of_codes():
    e, c = np.zeros((128, 128, 4), np.float32), np.zeros((128, 2, 4), np.uint8)
    e[np.arange(128), np.arange(128), 0] = 1
    c[:127, :, 0] = np.arange(256).reshape(2, 128).T[:127]
    return mx_ref.matmul(mx_ref.quantize(e.reshape(128, 512).astype(BF)), (c.reshape(128, 8), np.full((16, 2), 127, np.uint8))).T.reshape(-1).astype(np.float64)
CODE_VALUE, SCALE_VALUE = values_of_codes(), 2.0 ** (np.arange(256) - 127.0)
def decode(q):
    return (CODE_VALUE[q[0]].reshape(16, 8, -1, 4) * SCALE_VALUE[q[1]][:, None, :, None] + 0.0).reshape(128, -1).astype(np.float32)
def f(rng, *shape):
    return mx_ref.flush((rng.standard_normal(shape, dtype=np.float32) * np.exp2(rng.integers(-2, 3, shape[:-1] + (1,)))).astype(BF))
def wide(rng, *shape, cols=0):
    v = rng.standard_normal(shape, dtype=np.float32) * np.exp2(rng.integers(-12, 13, shape)).astype(np.float32)
    if cols: v *= np.repeat(np.exp2(rng.integers(-cols, cols + 1, shape[:-2] + (1, shape[-1] // 4))) * (rng.random(shape[:-2] + (1, shape[-1] // 4)) > 0.0625), 4, axis=-1).astype(np.float32)
    return mx_ref.flush(v.astype(BF))
C, R = 384, 2
SETS = np.arange(256)
ONE = (1 << np.arange(8))[:, None]
DECIDE = [16 * g + k for g in range(8) for k in range(10)] + [15]
def bits(b):
    return np.packbits(b, axis=-2, bitorder="little")[..., 0, :].astype(np.int64)
def numbers_of(rng):
    return {"x": np.array(f(rng, N, 128, 4 * C)), "u": np.array(f(rng, N, 128, 512)), "v": np.array(f(rng, N, 128, 512))}
def same(rng, w):
    c, s = packed(np.stack([w] * N), rng)
    return {"wc": c, "ws": np.stack([s[0]] * N)}
def weights(rng, keep=np.ones((8, 16), bool)):
    w = f(rng, 128, 2048).astype(np.float32).reshape(8, 16, 4, 8, 16, 4)
    w = np.where(keep[:, :, None, None, None, None] & keep[:, :, None], w, np.float32(0.0))
    return same(rng, w.reshape(128, 2048).astype(BF))
def setup_inputs(rng):
    return {**numbers_of(rng), **weights(rng)}
def setup_inputs_ties(rng):
    d = numbers_of(rng)
    e = rng.permutation(N)
    x = d["x"].reshape(N, 8, 16, C, 4)
    x[:, :, 0] = rng.integers(0, 3, (N, 8, C, 4)).astype(np.float32).astype(BF)
    x[e[0], 0, 0, :, 3] = 2.0
    x[e[1]] = 0.0
    u = d["u"].reshape(N, 128, 128, 4)
    u[:, :, DECIDE] = 0.0
    for g in range(8):
        u[:, 16 * g, 16 * g, 0] = 1.0
        u[:, 16 * g, 16 * g + 1, 1] = 1.0
        for k in range(8): u[:, 16 * ((g + k) % 8), 16 * g + 2 + k, 2] = 1.0
    u[:, 0, 15, 3] = 1.0
    u[e[2], 0, 15, 3] = -1.0
    keep = np.ones((8, 16), bool)
    keep[:, 0] = False
    return {"x": x.reshape(N, 128, 4 * C), "u": u.reshape(N, 128, 512), "v": d["v"], **weights(rng, keep)}
def setup_inputs_near(rng):
    d = numbers_of(rng)
    x = d["x"].astype(np.float32).reshape(N, 8, 16, C, 4)
    digits = lambda a: ((a[..., None] >> np.arange(4)) & 1) * np.exp2(np.arange(4) - 23.0)
    o = rng.permutation(N)
    n = rng.integers(0, 16, (N, 8, 3, C))
    far = []
    for r in range(N):
        if o[r] % 2 == 0:
            j, g = int(rng.integers(C)), int(rng.integers(5))
            n[r, :, 0, j] = 0
            n[r, g, 0, j] = 15
            n[r, g, 1, j] = 0
            far.append((r, j))
    have = n[:, :, 0] > n[:, :, 1]
    kind = np.where(have[:, 7], np.where(have[:, 6], 2, 1), 0)
    s = digits(2 * (7 - np.count_nonzero(have[:, :7], axis=1)) + rng.integers(0, 2, (N, C)))
    x[:, :, 8:] = 0
    x[:, 5:, :8] = 0
    x[:, :, 8:11] = digits(n)
    x[:, :, 11, :, 0] = 2.0 ** -10
    x[:, 7, 0, :, 0] = 1.0
    for k in range(2):
        x[:, k, 12] = s * (kind == k)[:, :, None]
        x[:, k, 13, :, 0] = (kind == k) * 2.0 ** -10
        x[:, 7 - k, 1, :, 0] = kind == k
    x[:, 5, 1, :, 0] = np.where(kind == 2, -(1.0 + 0.125 * rng.integers(0, 3, (N, C))) * 2.0 ** -30, 0.0)
    for r, j in far: x[r, 7, 1, j, 0] = 2.0 ** 30
    u = d["u"].reshape(N, 128, 128, 4)
    u[:, :, DECIDE] = 0.0
    for r in range(N):
        k = 2.0 ** -30 if o[r] < N // 2 else 1.0
        for g in range(8):
            for i in range(10):
                h = 16 * g + i
                u[r, 112, h, 0] = k
                u[r, 16 * g + 11, h, 0] = k
                u[r, 16 * g + 8 + i if i < 2 else 16 * ((g + i - 2) % 8) + 10, h] = k
    for p, k in ((113, 1.0), (13, 1.0), (97, 2.0 ** -30), (29, 2.0 ** -30), (81, 2.0 ** -30)): u[:, p, 15, 0] = k
    u[:, 12, 15] = 1.0
    u[:, 28, 15] = 2.0 ** -30
    keep = np.zeros((8, 16), bool)
    keep[:5, :8] = True
    return {"x": x.reshape(N, 128, 4 * C).astype(BF), "u": u.reshape(N, 128, 512), "v": d["v"], **weights(rng, keep)}
def setup_inputs_huge(rng):
    d = numbers_of(rng)
    c = rng.integers(0, 2, (N, 1, 1, C, 1)) * 2.0 - 1.0
    x = (0.9 + 0.05 * rng.random((N, 8, 16, C, 4))) * 2.0 ** 30 * c
    u = d["u"].reshape(N, 128, 128, 4)
    u[:, :, DECIDE] = 0.0
    for r in range(N):
        for h in DECIDE[:-1]: u[r, rng.permutation(128)[:64], h] = 2.0 ** 30
        u[r, :, 112] = 0.0
        u[r, :, 15] = (2.0 ** 30 * (1.0 - 0.03 * rng.random((128, 4)))).astype(np.float32).astype(BF)
    w = np.zeros((128, 4, 128, 4), np.float32)
    i = np.arange(128)
    for b in range(4): w[i, b, i, b] = -0.5
    return {"x": x.astype(np.float32).reshape(N, 128, 4 * C).astype(BF), "u": u.reshape(N, 128, 512), "v": d["v"], **same(rng, w.reshape(128, 2048).astype(BF))}
def setup_inputs_few(rng):
    d = numbers_of(rng)
    e = rng.permutation(N)
    x = d["x"].reshape(N, 8, 16, C, 4)
    k = (1.0 + (2 * rng.integers(0, 64, (N, 8, 8, C, 4)) + 1) * 2.0 ** -7) * np.exp2(-rng.integers(8, 15, (N, 8, 8, C, 4)).astype(np.float32))
    x[:, :, 8:] = (k * rng.choice([-1.0, 1.0], (N, 8, 8, C, 4))).astype(np.float32).astype(BF)
    x[:, :, 8, :, 0] = 1.96875
    have = rng.random((N, 8, C)) < 0.5
    have[e[0]] = True
    have[e[1]] = False
    have[e[2]] = np.arange(8)[:, None] == rng.integers(0, 7, C)
    j = int(rng.integers(C))
    have[e[3], 0, j] = False
    have[e[3], 1:, j] = True
    have[:, 7] = False
    x[:, :, 0, :, 0] = np.where(have, 1.0, -1.0).astype(np.float32).astype(BF)
    x[e[3], 0, 2, :, 0] = np.where(have[e[3], 0], -1.0, 1.0).astype(np.float32).astype(BF)
    s = rng.integers(-8, 9, (N, C))
    s[e[0]] = 64 + 8 * rng.integers(0, 8, C)
    s[e[0], C - 1] = 128
    x[:, 0, 1, :, 0] = s.astype(np.float32).astype(BF)
    u = d["u"].reshape(N, 128, 128, 4)
    u[:, :, ::16] = 0.0
    u[:, :, 1::16] = 0.0
    u[:, :, 15] = 0.0
    for h in range(0, 128, 16): u[:, h, h, 0] = 1.0
    u[:, 1, 15, 0] = 1.0
    u[e[3], 112, 112, 0] = 0.0
    u[e[3], 2, 112, 0] = 1.0
    u[e[3], :, 9] = 0.0
    w = f(rng, 128, 2048).astype(np.float32).reshape(8, 16, 4, 8, 16, 4)
    w[:, :, :, :, 8:] = 0
    i = np.arange(8)
    for p in range(8, 16):
        for b in range(4): w[i, p, b, i, p, b] = 32.0
    w[:, 8, 0, :, 8, 0] = 0
    w[:, :, 0, 0, 2] = 0
    w[0, 0, 0, 0, 2, 0] = -64.0
    w[:, :, 0, 7, 0] = 0
    return {"x": x.reshape(N, 128, 4 * C), "u": u.reshape(N, 128, 512), "v": d["v"], **same(rng, w.reshape(128, 2048).astype(BF))}
def setup_inputs_spread(rng):
    d = setup_inputs(rng)
    d["x"] = wide(rng, N, 128, 4 * C, cols=6)
    return d
def check_inputs(d):
    b = []
    for k in ("x", "u", "v"):
        a = np.abs(d[k].astype(np.float32))
        if not (np.isfinite(a).all() and ((a == 0) | (a >= 2.0 ** -30) & (a <= 2.0 ** 30)).all()): b.append("a value of " + k)
    if ((d["wc"] & 0x7F) == 0x7F).any(): b.append("a code of wc that is no number")
    for k in ("wc", "ws"):
        if (d[k] != d[k][:1]).any(): b.append(k + " isn't the same on all ranks")
    none, least, most = [emit(mx_ref.quantize(np.full((128, 16), k, np.float32).astype(BF)))[1][0, 0] for k in (0.0, 2.0 ** -30, 2.0 ** 30)]
    for r in range(N):
        a = mx_ref.live(d["ws"][r])
        if not ((a == none) | (a >= least) & (a <= most)).all(): b.append("a scale of ws")
    return b
def reference(x, u, v, wc, ws):
    qu = [mx_ref.quantize(u[r]) for r in range(N)]
    lay = pk(wc[0], ws[0])
    now = [x[r] for r in range(N)]
    for t in range(R):
        q = [mx_ref.quantize(now[r]) for r in range(N)]
        best, rep = np.zeros((N, 256), np.float32), np.zeros((N, 256), np.int64)
        here, want = np.zeros((N, 8, C), bool), np.zeros((N, 8, C), np.int64)
        for r in range(N):
            s = mx_ref.matmul(qu[r], q[r]) + np.float32(0.0)
            a = s.reshape(8, 16, C)
            here[r] = a[:, 0] > a[:, 1]
            m = bits(here[r])
            want[r] = (m & bits(a[:, 2:10] > a[:, 1:2])) | ONE
            holds = (m & SETS[:, None]) == SETS[:, None]
            strong = np.where(holds, s[15], np.float32(-np.inf))
            rep[r] = np.argmax(strong, axis=1)
            best[r] = np.max(strong, axis=1)
        win = np.argmax(best, axis=0)
        got = pick(join(*q), np.where(np.isfinite(best[win, SETS]), C * win + rep[win, SETS], -1))
        made = tile([mx_ref.matmul(pick(lay, np.arange(128 * b, 128 * b + 128)), got) * np.float32(0.03125) for b in range(4)])
        table = decode(mx_ref.quantize(made)).astype(BF)
        for r in range(N):
            now[r] = (now[r].astype(np.float32) + gcols(table, np.where(here[r], -1, want[r])).astype(np.float32)).astype(BF)
    y, wl = np.zeros((N, 128, C), np.float32), np.zeros((N, 8, C), np.float32)
    oc, osc = np.zeros((N, 128, 4 * C), np.uint8), np.zeros((N, 16, C), np.uint8)
    for r in range(N):
        q = mx_ref.quantize(now[r])
        y[r] = mx_ref.matmul(mx_ref.quantize(v[r]), q)
        wl[r] = want[r]
        oc[r], osc[r] = emit(q)
    return {"y": y, "wl": wl, "oc": oc, "osc": osc}

@@ -1,0 +1,543 @@
+from concourse.bass import DstId, RemoteDMATransfer
+from concourse.mybir import dt, AluOpType, ActivationFunctionType, AxisListType
+
+ALU, ACT = AluOpType, ActivationFunctionType
+NR = 8
+C = 384
+BIG = 2.0 ** 30
+
+
+def _scratch():
+    s = {}
+
+    def bf(name, n): s[name] = ("sbuf", [128, n], "bfloat16")
+    def f32(name, n): s[name] = ("sbuf", [128, n], "float32")
+    def i32(name, n): s[name] = ("sbuf", [128, n], "int32")
+    def u16(name, n): s[name] = ("sbuf", [128, n], "uint16")
+
+    def mx(name, n):
+        s[name] = ("sbuf", [128, n], "float8_e4m3fn_x4")
+        s[name + "s"] = ("sbuf", [128, n], "uint8")
+
+    bf("ut", 512); bf("vt", 512)
+    for t in range(3):
+        bf("x%d" % t, 4 * C); mx("qx%d" % t, C)
+    bf("ab", 4 * C); bf("hc", 1024); bf("zt", 512); bf("z", 1024); bf("ht", 512); bf("pr", 512)
+    bf("ct", 3584); bf("yt", 1024); bf("pf", C); bf("wf", C); bf("sj", 2 * C); bf("wzi", 512)
+    f32("pth", C); f32("ath", C); f32("s15", C); f32("mk", 2 * C); f32("ix", 2); f32("fc", 64); f32("m8", 8); f32("ni", 8)
+    f32("lf", 96); f32("yo", C); f32("wlb", C); f32("mi", 128); f32("fi", 512); f32("gw", 512); f32("et", 1024)
+    f32("wn", 32); f32("wt", 128); f32("wm", 32); f32("wi", 32); f32("la", 24)
+    i32("ic", 16); i32("jc", 16); i32("mj", 128); i32("lu", 16); i32("ai", 16); i32("dg", 64)
+    u16("lup", 24); u16("lua", 16); u16("ls", 16); u16("off", 96)
+    mx("uq", 128); mx("up", 384); mx("ua", 256); mx("vq", 128); mx("wq", 512); mx("qab", C); mx("qhc", 256); mx("zq", 128)
+    mx("qz", 256); mx("qpr", 128); mx("qc", 896)
+    for t in range(2):
+        k = str(t)
+        f32("rm" + k, 2 * C); f32("stl" + k, 32); f32("rst" + k, 1); u16("tl" + k, 2)
+        mx("ca" + k, 128); mx("cb" + k, 128); mx("land" + k, 288); mx("tq" + k, 128); mx("qh" + k, 128); mx("yq" + k, 256)
+        mx("rp" + k, 64); mx("ry" + k, 32)
+    for b in range(8):
+        s["b%d" % b] = ("psum", [128, 512], "float32")
+    return s
+
+
+SCRATCH = _scratch()
+_REMOTE = ["st", "pc", "ps", "yco", "yso", "ycx", "ysx"]
+_RSEMS = [n + str(t) for t in range(2) for n in _REMOTE] + ["lr"]
+SEMAPHORES = _RSEMS + ["c%d" % i for i in range(135)]
+
+
+def _m(engines):
+    return sum(1 << e for e in engines)
+
+
+def _plan(T, topo):
+    cs = list(T.cores)
+    par = [0 if r == 0 or topo.may_write(cs[0], cs[r]) else 1 for r in range(NR)]
+    own = [[s for s in range(NR) if par[s] == par[r]] for r in range(NR)]
+    cross = [[s for s in range(NR) if par[s] != par[r]] for r in range(NR)]
+    kk = [own[r].index(r) for r in range(NR)]
+    relay = []
+    for r in range(NR):
+        can = [c for c in topo.cores_of(cs[r]) if c != cs[r] and all(topo.may_write(c, cs[d]) for d in cross[r])]
+        near = [c for c in can if topo.die(c) == topo.die(cs[r])]
+        far = [c for c in can if topo.die(c) != topo.die(cs[r])]
+        a, b = (near, far) if kk[r] % 2 == 0 else (far, near)
+        relay.append([(a[0], 0, 0), (b[0], 2, 0), (a[1], 0, 1), (b[1], 2, 1)])
+    return cs, par, own, cross, kk, relay
+
+
+def _dst(topo, d, core):
+    rid, pid = topo.addr(d, core)
+    return DstId(rid=rid, pnc=pid)
+
+
+def _direct(topo, r, d, cs, own):
+    o = [s for s in own[r] if s != r]
+    e = topo.engines(cs[r], cs[d])
+    i = o.index(d)
+    return (e[0:4], e[4:6], e[6:8])[i], (e[0:2], e[2:4], e[4:8])[i]
+
+
+def _relay_program(g, core, T, topo, r, first, role, plan):
+    cs, par, own, cross, kk, relay = plan
+    d0, d1 = cross[r][first], cross[r][first + 1]
+    eng = topo.engines(core, cs[d0])
+    ids = [_dst(topo, cs[d], core) for d in (d0, d1)]
+    loc = [0]
+    what = "s" if role else ""
+
+    def u8(v):
+        return v if role else v.bitcast(dt.uint8)
+
+    def send(trs, n):
+        g.remote_dma_fused(trs, local_sem=T.sem.lr)
+        loc[0] += n
+
+    for t in range(2):
+        k = str(t)
+        sm = T.sem["st" + k]
+        g.wait_ge(sm, 8)
+        send([RemoteDMATransfer(dst_ids=[ids[role]], dma_engine_mask=_m(eng), remote_sem=sm, srcs=[T["rst" + k][:]], dsts=[T["stl" + k][:, 4 * r:4 * r + 1]])], len(eng))
+        sm = T.sem[("ps" if role else "pc") + k]
+        g.wait_ge(sm, 8)
+        half = [eng[0:4], eng[4:8]]
+        send([RemoteDMATransfer(dst_ids=[ids[i]], dma_engine_mask=_m(half[i]), remote_sem=sm, srcs=[u8(T["rp" + k + what][:, 32 * i:32 * i + 32])],
+                                dsts=[u8(T["land" + k + what][:, 32 * r:32 * r + 32])]) for i in range(2)], len(eng))
+        a = 128 * par[r] + 32 * kk[r]
+        sm = T.sem[("ysx" if role else "ycx") + k]
+        g.wait_ge(sm, 8 if role else 16)
+        d = T["yq" + k + what]
+        send([RemoteDMATransfer(dst_ids=ids, dma_engine_mask=_m(eng), remote_sem=sm, srcs=[u8(T["ry" + k + what][:, 0:32])],
+                                dsts=[u8(d[:, a:a + 32]), u8(d[:, a:a + 32])])], len(eng))
+    g.wait_ge(T.sem.lr, loc[0])
+
+
+def rank_program(g, core, T, topo):
+    plan = _plan(T, topo)
+    rank = T.rank_of(core)
+    if rank is None:
+        for r in range(NR):
+            for c, first, role in plan[5][r]:
+                if c == core:
+                    _relay_program(g, core, T, topo, r, first, role, plan)
+        return
+    _rank_program(g, core, T, topo, rank, plan)
+
+
+def _rank_program(g, core, T, topo, r, plan):
+    cs, par, own, cross, kk, relay = plan
+    me, mk = par[r], kk[r]
+    peers = [s for s in own[r] if s != r]
+    V, S, P = g.vector, g.scalar, g.tensor
+    names, cnt, seen, done = {}, {}, {}, {}
+    bank = [T["b%d" % i] for i in range(8)]
+    qid = {"g": g, "v": V, "s": S, "p": P, "q": g.sync}
+
+    def sem(label):
+        if label in _RSEMS:
+            return T.sem[label]
+        if label not in names:
+            names[label] = "c%d" % len(names)
+        return T.sem[names[label]]
+
+    def w(q, *labels):
+        for lb in labels:
+            n = cnt.get(lb, 0)
+            if n and seen.get((q, lb), 0) < n:
+                qid[q].wait_ge(sem(lb), n)
+                seen[(q, lb)] = n
+                done[lb] = max(done.get(lb, 0), n)
+
+    def do(q, label, deps, method, *args, **kw):
+        w(q, *deps)
+        n = kw.pop("n", 1)
+        method(*args, **kw).then_inc(sem(label), n)
+        cnt[label] = cnt.get(label, 0) + n
+
+    def dma(q, label, deps, out, in_):
+        do(q, label, deps, qid[q].dma_start, out, in_, n=16)
+
+    def ts(label, deps, out, in0, s1, op0, s2=None, op1=None):
+        if op1 is None:
+            do("v", label, deps, V.tensor_scalar, out, in0, s1, None, op0)
+        else:
+            do("v", label, deps, V.tensor_scalar, out, in0, s1, s2, op0, op1)
+
+    def mm(label, deps, out, lhs, la, rhs, ra, rb):
+        do("p", label, deps, P.matmul_mx, out, T[lhs][:, la:la + 128], T[lhs + "s"][:, la:la + 128], T[rhs][:, ra:rb], T[rhs + "s"][:, ra:rb], True, True)
+
+    def quant(label, deps, out, a, b, tile, ta):
+        do("v", label, deps, V.quantize_mx, T[out][:, a:b], T[out + "s"][:, a:b], T[tile][:, ta:ta + 4 * (b - a)])
+
+    def pick(label, deps, out, a, b, win, wa, wb, off, e, f):
+        do("v", label + "c", deps, V.tensor_copy, T[out][:, a:b].bitcast(dt.uint32), T[win][:, wa:wb].bitcast(dt.uint32).indirect(T[off][:, e:f]))
+        do("s", label + "s", deps, S.activation, T[out + "s"][:, a:b], T[win + "s"][:, wa:wb].indirect(T[off][:, e:f]), ACT.Copy)
+
+    def act(label, deps, out, in_, func=ACT.Copy, **kw):
+        do("s", label, deps, S.activation, out, in_, func, **kw)
+
+    def send(masks, deps, trs):
+        w("g", *deps)
+        g.remote_dma_fused(trs, local_sem=T.sem.lr)
+        cnt["lr"] = cnt.get("lr", 0) + sum(bin(m).count("1") for m in masks)
+
+    def u8(name, what, a, b):
+        v = T[name + what][:, a:b]
+        return v if what else v.bitcast(dt.uint8)
+
+    def iota(label, out, pattern, base, ch, whole=False):
+        if whole:
+            do("g", label, [], g.iota, out, pattern, base, ch)
+        else:
+            do("g", label, [], g.iota, out, pattern, base, ch, allow_small_or_imprecise_dtypes=True)
+
+    fc = T.fc
+
+    def F(a, n=1):
+        return fc[:, a:a + n]
+
+    dma("q", "Lu", [], T.ut[:], T.u[:])
+    dma("s", "Lx0", [], T.x0[:, 0:768], T.x[:, 0:768])
+    dma("q", "Lx1", [], T.x0[:, 768:1536], T.x[:, 768:1536])
+    dma("q", "Lw", ["Lx0", "Lx1"], T.wqs[:], T.ws[:])
+    dma("q", "Lw", [], T.wq[:].bitcast(dt.uint8), T.wc[:])
+    dma("q", "Lv", [], T.vt[:], T.v[:])
+
+    iota("gl", T.lu[:], [[1, 2], [0, 8]], 0, 16, True)
+    iota("gp", T.ic[:], [[0, 16]], 0, 1, True)
+    iota("gm", T.mi[:], [[1, 128]], 0, 0)
+    iota("gn", T.ni[:], [[1, 8]], 0, 0)
+    iota("gz", T.wzi[:], [[0, 8], [1, 16], [0, 4]], 0, 0)
+    iota("kz", T.z[:], [[0, 1024]], 0, 0)
+    iota("gf", T.fi[:], [[1, 512]], 0, 0)
+    iota("gf", T.wi[:], [[1, 16], [0, 2]], 0, 0)
+    iota("gf", T.gw[:], [[1, 32], [0, 4], [-1, 4]], 0, 0)
+
+    do("v", "kzt", [], V.memset, T.zt[:], 0.0)
+    for i in range(2):
+        act("khm", ["kzt"], T.hc[:, 512 * i:512 * i + 512], T.zt[:])
+    for i in range(2):
+        act("kab", [], T.ab[:, 512 * i:512 * i + 512], T.zt[:])
+    do("v", "kl", [], V.memset, T.lup[:, 16:24], 15)
+    ts("kl", ["gl"], T.lu[:], T.lu[:], 113, ALU.bitwise_and)
+    do("v", "kl", ["kl"], V.tensor_copy, T.lup[:, 0:16], T.lu[:])
+
+    def jbits(*specs):
+        for col, shift, mask in specs:
+            out, in0 = T.jc[:, col:col + 1], T.ic[:, 0:1]
+            if shift and mask:
+                ts("kj", ["gp"], out, in0, shift, ALU.logical_shift_right, mask, ALU.bitwise_and)
+            elif shift:
+                ts("kj", ["gp"], out, in0, shift, ALU.logical_shift_right)
+            else:
+                ts("kj", ["gp"], out, in0, mask, ALU.bitwise_and)
+
+    jbits((0, 0, 7), (2, 0, 1), (4, 1, 1), (6, 2, 1), (9, 5, 0), (10, 1, 15))
+    do("v", "kf", ["kj"], V.tensor_copy, fc[:, 0:8:2], T.jc[:, 0:8:2])
+    do("v", "kf", [], V.tensor_copy, fc[:, 9:11], T.jc[:, 9:11])
+    ts("k1", ["kf"], F(24), F(2), -1.0, ALU.mult, 2.0, ALU.add)
+    ts("k1", [], F(25), F(4), -3.0, ALU.mult, 4.0, ALU.add)
+    ts("k1", [], F(26), F(6), -15.0, ALU.mult, 16.0, ALU.add)
+    ts("k1", [], F(29), F(9), 2.0, ALU.mult, F(2), ALU.add)
+    ts("k1", [], F(23), F(0), 7.0, ALU.is_equal, 128.0, ALU.mult)
+    ts("k1", [], F(57), F(10), -1.0, ALU.mult)
+    ts("k1", ["k1"], F(27), F(24), F(25), ALU.mult, F(26), ALU.mult)
+    ts("k1", ["k1", "gm"], T.mj[:], T.mi[:], F(27), ALU.mult)
+    ts("k1", ["k1"], T.mj[:], T.mj[:], 128, ALU.bitwise_and)
+    w("v", "k1", "khm")
+    for h in range(2):
+        out = T.hc[:, 512 * h:512 * h + 512:4]
+        if (me if h else 1 - me):
+            ts("k1", [], out, T.mj[:], F(23), ALU.add, -BIG / 128, ALU.mult)
+        else:
+            ts("k1", [], out, T.mj[:], -BIG / 128, ALU.mult)
+    quant("uq", ["Lu"], "uq", 0, 128, "ut", 0)
+    pick("up", ["uq", "kl"], "up", 0, 256, "uq", 0, 128, "lup", 0, 16)
+    quant("qx0", ["Lx0"], "qx0", 0, 192, "x0", 0)
+    quant("qx1", ["Lx1"], "qx0", 192, 384, "x0", 768)
+    act("kab", [], T.ab[:, 1024:1536], T.zt[:])
+    pick("u5", [], "up", 256, 384, "uq", 0, 128, "lup", 16, 24)
+    quant("qhc", ["k1"], "qhc", 0, 256, "hc", 0)
+    quant("zq", ["kzt"], "zq", 0, 128, "zt", 0)
+    for t in range(2):
+        for what in ("", "s"):
+            dma("q", "kland", ["zq"], u8("land%d" % t, what, 256, 288), u8("zq", what, 0, 32))
+            dma("q", "kland", ["zq"], u8("tq%d" % t, what, 32, 128), u8("zq", what, 32, 128))
+
+    def consts_a():
+        jbits((1, 4, 0), (3, 4, 1), (5, 5, 1), (7, 6, 1), (8, 3, 1), (11, 0, 3), (12, 0, 127), (14, 0, 15))
+        do("v", "kf", ["kj"], V.tensor_copy, fc[:, 1:8:2], T.jc[:, 1:8:2])
+        do("v", "kf", [], V.tensor_copy, F(8), T.jc[:, 8:9])
+        do("v", "kf", [], V.tensor_copy, F(11, 2), T.jc[:, 11:13])
+        do("v", "kf", [], V.tensor_copy, F(22), T.jc[:, 14:15])
+        ts("km8", ["kf"], F(30), F(12), 4.0, ALU.mult)
+        ts("kc", [], F(31), F(2), 16.0, ALU.mult, F(10), ALU.add)
+        if me == 0 and mk == 0:
+            ts("kwt", [], F(15), F(12), 0.0, ALU.is_equal, 2.0 ** 81, ALU.mult)
+            ts("kc", ["kwt"], F(32), F(15), -2.0 ** 50, ALU.add)
+        else:
+            do("v", "kc", [], V.memset, F(32), -2.0 ** 50)
+        do("v", "kwt", [], V.memset, T.wt[:, 0:32], 0.0)
+        ts("kwt", ["gf"], T.wm[:], T.wi[:], F(22), ALU.is_equal)
+        for b in range(4):
+            ts("ke0", ["km8"], F((28, 43, 55, 56)[b]), F(30), -1.0, ALU.mult, -float(b), ALU.add)
+        do("v", "kht", [], V.memset, T.ht[:], 0.0)
+        do("v", "kht", [], V.memset, T.pr[:, 384:512], 0.0)
+        unpackers(2)
+        unpackers(3)
+
+    def unpackers(b, stage=2):
+        e = T.et[:, 512 * (b % 2):512 * (b % 2) + 512]
+        if stage != 1:
+            act("kes", ["ke0", "gf"], e, T.fi[:], ACT.Abs, bias=F((28, 43, 55, 56)[b]))
+        if stage:
+            act("kes", ["kes"], T.ct[:, 1536 + 512 * b:2048 + 512 * b], e, ACT.Relu, bias=1.0, scale=-1.0)
+
+    def consts_b1():
+        ts("kn", [], F(18, 2), F(2, 2), 1.0, ALU.add)
+        ts("kn", [], F(20, 2), F(4, 2), 3.0, ALU.mult, 1.0, ALU.add)
+        ts("kn", [], F(13), F(6), 15.0, ALU.mult, 1.0, ALU.add)
+        ts("kn", [], F(14), F(7), 15.0, ALU.mult, 1.0, ALU.add)
+        ts("kn", [], F(35, 2), F(0, 2), 5.0, ALU.is_ge, 0.5, ALU.mult)
+        ts("kn", [], F(37, 2), F(0, 2), 0.0, ALU.is_equal, 15.5, ALU.mult)
+        ts("kn", [], F(44), F(0), 2.0, ALU.add)
+        ts("kn", [], F(45), F(0), F(1), ALU.not_equal)
+        ts("kn", [], F(46), F(8), -1.0, ALU.mult, 1.0, ALU.add)
+        ts("kn", [], F(54), F(1), 4.0, ALU.mult)
+        ts("kn", [], T.la[:, 0:8], T.ni[:], 16.0, ALU.mult)
+
+    def consts_b2():
+        do("v", "kn", ["kn"], V.tensor_tensor, F(33, 2), F(18, 2), F(20, 2), ALU.mult)
+        ts("kn", [], F(39, 2), F(35, 2), 0.5, ALU.add)
+        ts("kn", [], F(58, 6), T.ni[:, 0:6], F(0), ALU.not_equal, F(44), ALU.mult)
+        ts("kn", [], T.wn[:, 30:32], T.ni[:, 6:8], F(0), ALU.not_equal, F(44), ALU.mult)
+        ts("kn", [], T.la[:, 16:24], T.la[:, 0:8], 1.0, ALU.add)
+
+    def consts_b3():
+        do("v", "kn", ["kn"], V.tensor_tensor, F(16, 2), F(33, 2), F(13, 2), ALU.mult)
+        do("v", "kn", [], V.tensor_tensor, T.la[:, 8:14], F(58, 6), T.la[:, 0:6], ALU.add)
+        do("v", "kn", [], V.tensor_tensor, T.la[:, 14:16], T.wn[:, 30:32], T.la[:, 6:8], ALU.add)
+        do("v", "kn", ["kn"], V.tensor_tensor, F(41, 2), F(39, 2), F(16, 2), ALU.mult)
+        ts("kn", [], F(51), F(45), F(16), ALU.mult, F(46), ALU.mult)
+        do("v", "kla", [], V.tensor_copy, T.lua[:], T.la[:, 8:24])
+        do("v", "kn", ["kn"], V.tensor_tensor, F(47, 2), F(41, 2), F(37, 2), ALU.add)
+        ts("kn", ["kn"], F(49), F(47), 4.0, ALU.mult, 1024.0, ALU.add)
+        ts("kn", [], F(50), F(48), 4.0, ALU.mult, F(11), ALU.add)
+        ts("kn", ["kn"], F(52), F(49), F(45), ALU.mult, 1024.0, ALU.subtract)
+        ts("kn", ["kn"], F(53), F(52), F(46), ALU.mult)
+
+    def consts_c():
+        pick("ua", ["kla"], "ua", 0, 256, "uq", 0, 128, "lua", 0, 16)
+        ts("kw", ["gf", "kn"], T.ct[:, 512:1024], T.gw[:], F(54), ALU.is_equal, F(53), ALU.mult)
+        quant("qwl", ["kw"], "qc", 128, 256, "ct", 512)
+
+    def consts_d():
+        ts("kv", [], T.ct[:, 1024:1536], T.fi[:], F(54), ALU.is_equal, F(51), ALU.mult)
+        quant("qww", ["kv"], "qc", 256, 384, "ct", 1024)
+        quant("vq", ["Lv"], "vq", 0, 128, "vt", 0)
+
+    codes_to, scales_to = relay[r][0:2], relay[r][2:4]
+    e_off = topo.engines(core, cs[peers[0]])
+    e_on = [e for e in topo.engines(core, codes_to[0][0]) if e not in e_off]
+    rid = {"": [_dst(topo, c[0], core) for c in codes_to], "s": [_dst(topo, c[0], core) for c in scales_to]}
+    pid = [_dst(topo, cs[d], core) for d in peers]
+
+    for t in range(2):
+        k = str(t)
+        qx, x, xn = "qx" + k, T["x" + k], T["x%d" % (t + 1)]
+        rm = T["rm" + k]
+        for i in range(2):
+            lo, hi = 192 * i, 192 * i + 192
+            mm("mpt%d" % i, ["qx%d" % i, "upc", "ups"], bank[(1, 4)[i]][:, 0:192], "up", 128, qx, lo, hi)
+            mm("mp%d" % i, [], bank[(0, 3)[i]][:, 0:192], "up", 0, qx, lo, hi)
+            act("pth%d" % i, ["mpt%d" % i], T.pth[:, lo:hi], bank[(1, 4)[i]][:, 0:192])
+        mm("ms", ["u5c", "u5s"], bank[2][:, 0:C], "up", 256, qx, 0, C)
+        act("s15", ["ms"], T.s15[:], bank[2][:, 0:C], scale=1.0 / BIG)
+        if t == 0:
+            act("kwz", ["gz", "k1"], T.et[:, 0:512], T.wzi[:], ACT.Abs, bias=F(57))
+            act("kwz", ["kwz"], T.ct[:, 0:512], T.et[:, 0:512], ACT.Relu, bias=1.0, scale=-1.0)
+        for i in range(2):
+            lo, hi = 192 * i, 192 * i + 192
+            do("v", "pf%d" % i, ["mp%d" % i, "pth%d" % i], V.tensor_tensor, T.pf[:, lo:hi], bank[(0, 3)[i]][:, 0:192], T.pth[:, lo:hi], ALU.is_le)
+            if i:
+                quant("qab", ["ab"], "qab", 0, 192, "ab", 0)
+            ts("ab", ["pf%d" % i, "kab"], T.ab[:, 4 * lo:4 * hi:4], T.pf[:, lo:hi], BIG, ALU.mult)
+        quant("qab", ["ab"], "qab", 192, 384, "ab", 768)
+        for h in range(2):
+            mm("mc%d" % h, ["qab", "qhc"], bank[5 + h][:, 0:C], "qhc", 128 * h, "qab", 0, C)
+
+        def scores():
+            mm("ma", ["uac", "uas", "pth0", "pth1"], bank[1][:, 0:C], "ua", 0, qx, 0, C)
+            mm("mat", ["s15"], bank[2][:, 0:C], "ua", 128, qx, 0, C)
+
+        if t == 0:
+            ts("km8", ["gn"], T.m8[:], T.ni[:], F(29), ALU.is_equal)
+            do("v", "km8", [], V.memset, T.dg[:], 0)
+        else:
+            scores()
+        for h in range(2):
+            hs = str(h)
+            mk_, rmh = T.mk[:, C * h:C * h + C], rm[:, C * h:C * h + C]
+            last, sj = rm[:, C * h + C - 1:C * h + C], T.sj[:, C * h:C * h + C]
+            do("v", "mk" + hs, ["mc" + hs, "s15"], V.tensor_tensor, mk_, bank[5 + h][:, 0:C], T.s15[:], ALU.add)
+            do("v", "rm" + hs, ["mk" + hs], V.tensor_tensor_scan, rmh, mk_, mk_, -1e29, ALU.max, ALU.max)
+            act("ix" + hs, ["rm" + hs], sj, rmh, ACT.Sign, bias=last, scale=-1.0, accum_out=T.ix[:, h:h + 1])
+        if t == 0:
+            quant("qwz", ["kwz"], "qc", 0, 128, "ct", 0)
+        else:
+            act("ath", ["mat"], T.ath[:], bank[2][:, 0:C])
+        send([_m(e_on)], ["rm0"], [RemoteDMATransfer(dst_ids=rid[""] + rid["s"], dma_engine_mask=_m(e_on), remote_sem=T.sem["st" + k],
+                                                     srcs=[rm[:, C - 1:C]], dsts=[T["rst" + k][:] for i in range(4)])])
+        send([_m(e_off)], ["rm1"], [RemoteDMATransfer(dst_ids=pid, dma_engine_mask=_m(e_off), remote_sem=T.sem["st" + k], srcs=[rm[:, 2 * C - 1:2 * C]],
+                                                      dsts=[T["stl" + k][:, 4 * r:4 * r + 1] for d in peers])])
+
+        def digits(h):
+            hs, ai = str(h), T.ai[:, 8 * h:8 * h + 8]
+            ts("da" + hs, ["ix" + hs, "km8"], ai, T.m8[:], T.ix[:, h:h + 1], ALU.mult)
+            for b, ma in enumerate((448, 56, 7)):
+                ts("db" + hs, ["da" + hs], T.dg[:, 32 * h + b:32 * h + 32:4], ai, ma, ALU.bitwise_and)
+
+        def spread(h):
+            hs = str(h)
+            do("v", "dz" + hs, ["db" + hs, "kz"], V.tensor_copy, T.z[:, 512 * h:512 * h + 32], T.dg[:, 32 * h:32 * h + 32])
+            quant("qz" + hs, ["dz" + hs], "qz", 128 * h, 128 * h + 128, "z", 512 * h)
+            mm("mz" + hs, ["qz" + hs, "qwz"], bank[(7, 0)[h]][:, 0:128], "qc", 0, "qz", 128 * h, 128 * h + 128)
+
+        def choose(h):
+            hs = str(h)
+            do("v", "ls" + hs, ["mz" + hs], V.tensor_copy, T.ls[:, 8 * h:8 * h + 8], bank[(7, 0)[h]][:, 0:8])
+            pick("c" + hs, ["ls" + hs], ("ca", "cb")[h] + k, 0, 128, qx, 0, C, "ls", 8 * h, 8 * h + 8)
+
+        digits(0)
+        spread(0)
+        digits(1)
+        choose(0)
+        spread(1)
+        choose(1)
+        for what, sm, lb in (("", "pc", "c0c"), ("s", "ps", "c0s")):
+            ms = [_m(e_on), _m(e_off)]
+            send(ms, [lb], [RemoteDMATransfer(dst_ids=[rid[what][i]], dma_engine_mask=ms[i], remote_sem=T.sem[sm + k],
+                                              srcs=[u8("ca" + k, what, 32 * codes_to[i][1], 32 * codes_to[i][1] + 64)], dsts=[u8("rp" + k, what, 0, 64)]) for i in range(2)])
+        for what, sm, lb in (("", "pc", "c1c"), ("s", "ps", "c1s")):
+            ms = [_m(_direct(topo, r, d, cs, own)[1 if what else 0]) for d in peers]
+            send(ms, [lb], [RemoteDMATransfer(dst_ids=[pid[i]], dma_engine_mask=ms[i], remote_sem=T.sem[sm + k],
+                                              srcs=[u8("cb" + k, what, 32 * kk[d], 32 * kk[d] + 32)], dsts=[u8("land" + k, what, 32 * r, 32 * r + 32)]) for i, d in enumerate(peers)])
+        for what, lb in (("", "c1c"), ("s", "c1s")):
+            dma("q", "cown" + what, [lb], u8("land" + k, what, 32 * r, 32 * r + 32), u8("cb" + k, what, 32 * mk, 32 * mk + 32))
+        do("v", "sown", ["rm1"], V.tensor_copy, T["stl" + k][:, 4 * r:4 * r + 1], rm[:, 2 * C - 1:2 * C])
+
+        def wishes():
+            do("v", "wf", ["ma", "ath"], V.tensor_tensor, T.wf[:], bank[1][:, 0:C], T.ath[:], ALU.is_gt)
+            do("v", "pr", ["wf", "kht"], V.tensor_tensor, T.pr[:, 0:C], T.wf[:], T.pf[:], ALU.is_gt)
+
+        def offsets():
+            quant("qpr", ["pr"], "qpr", 0, 128, "pr", 0)
+            mm("ml", ["qpr", "qwl", "ls1"], bank[0][:, 0:128], "qc", 128, "qpr", 0, 128)
+            ts("lf", ["ml"], T.lf[:], bank[0][:, 0:96], F(50), ALU.add)
+            do("v", "off", ["lf"], V.tensor_copy, T.off[:], T.lf[:])
+
+        if t == 0:
+            consts_a()
+            consts_b1()
+        else:
+            wishes()
+        cnt["st" + k] = 8 * 3 + 8 * 4
+        wn, so = T.wn, T["stl" + k]
+        do("v", "w1", ["st" + k, "sown"], V.tensor_tensor_scan, wn[:, 0:8], so[:, 0:32:4], so[:, 0:32:4], -1e29, ALU.max, ALU.max)
+        ts("w1", ["w1"], wn[:, 8:16], wn[:, 0:8], wn[:, 7:8], ALU.is_lt, 32.0, ALU.mult)
+        ts("w1", ["kc"], wn[:, 18:19], wn[:, 7:8], F(32), ALU.is_lt, 256.0, ALU.mult)
+        do("v", "w1", ["w1"], V.tensor_reduce, wn[:, 16:17], wn[:, 8:16], AxisListType.X, ALU.add)
+        ts("w1", ["w1", "kwt"], T.wt[:, 0:1], wn[:, 16:17], F(31), ALU.add, wn[:, 18:19], ALU.max)
+        p0 = 32 * mk
+        do("v", "w2", ["w1"], V.transpose, T.wt[p0:p0 + 32, 32:64], T.wt[p0:p0 + 32, 0:32])
+        do("g", "w3", ["w2"], g.partition_broadcast, T.wt[:, 64:96], T.wt[p0:p0 + 1, 32:64], 128)
+        if t == 0:
+            consts_b2()
+        do("v", "w1", ["w3"], V.tensor_tensor, T.wt[:, 96:128], T.wt[:, 64:96], T.wm[:], ALU.mult)
+        for i in range(2):
+            do("v", "w4", ["w1"], V.tensor_reduce, wn[:, 20 + i:21 + i], T.wt[:, 96 + i:128:2], AxisListType.X, ALU.add)
+        do("v", "tl", ["w4"], V.tensor_copy, T["tl" + k][:], wn[:, 20:22])
+        cnt["pc" + k] = sum(len(_direct(topo, s, r, cs, own)[0]) for s in peers) + 16
+        cnt["ps" + k] = sum(len(_direct(topo, s, r, cs, own)[1]) for s in peers) + 16
+        win, tq = "land" + k, "tq" + k
+        w("v", "tl", "kland", "cown", "pc" + k)
+        w("s", "tl", "kland", "cowns", "ps" + k)
+        pick("t", [], tq, 0, 32, win, 0, 288, "tl" + k, 0, 2)
+        for b in range(4):
+            mm("mh%d" % b, ["tc", "ts", "Lw"], bank[3 + b][:, 0:128], "wq", 128 * b, tq, 0, 128)
+            if b != 1:
+                ts("hv", ["mh%d" % b, "kht"], T.ht[:, b:128:4], bank[3 + b][:, 0:32], 0.03125, ALU.mult)
+            else:
+                act("hs", ["mh%d" % b, "kht"], T.ht[:, b:128:4], bank[3 + b][:, 0:32], scale=0.03125)
+        qh = "qh" + k
+        quant("qh", ["hv", "hs"], qh, 0, 128, "ht", 0)
+        a = 128 * me + 32 * mk
+
+        def out(what, e):
+            return RemoteDMATransfer(dst_ids=rid[what], dma_engine_mask=_m(e), remote_sem=T.sem[("ysx" if what else "ycx") + k], srcs=[u8(qh, what, 0, 32)],
+                                     dsts=[u8("ry" + k, what, 0, 32) for i in range(2)])
+
+        def straight(what):
+            return RemoteDMATransfer(dst_ids=pid, dma_engine_mask=_m(e_off), remote_sem=T.sem[("yso" if what else "yco") + k], srcs=[u8(qh, what, 0, 32)],
+                                     dsts=[u8("yq" + k, what, a, a + 32) for d in peers])
+
+        send([_m(e_off + e_on)], ["qh"], [out("", e_off + e_on)])
+        send([_m(e_on), _m(e_off)], [], [out("s", e_on), straight("s")])
+        send([_m(e_off)], [], [straight("")])
+        for what in ("", "s"):
+            dma("q", "yown", ["qh"], u8("yq" + k, what, a, a + 32), u8(qh, what, 0, 32))
+        if t == 0:
+            consts_b3()
+            consts_c()
+            unpackers(0, 0)
+            scores()
+            act("ath", ["mat"], T.ath[:], bank[2][:, 0:C])
+            unpackers(0, 1)
+            unpackers(1)
+            wishes()
+            offsets()
+            quant("qe", ["kes"], "qc", 384, 896, "ct", 1536)
+        else:
+            offsets()
+            consts_d()
+            do("v", "pw", ["pr"], V.tensor_copy, T.ab[:, 0:4 * C:4], T.pr[:, 0:C])
+            quant("qpw", ["pw"], "qab", 0, C, "ab", 0)
+            mm("mw", ["qpw", "qww"], bank[7][:, 0:C], "qc", 256, "qab", 0, C)
+            ts("wlb", ["mw"], T.wlb[0:8, :], bank[7][0:8, 0:C], fc[0:8, 16:17], ALU.add)
+            dma("q", "so", ["wlb"], T.wl[:], T.wlb[0:8, :])
+        cnt["yco" + k] = cnt["yso" + k] = 24
+        cnt["ycx" + k] = cnt["ysx" + k] = 32
+        for i, (half, bb, deps) in enumerate(((me, (3, 4, 5, 6), ["qh", "qe", "yown", "yco" + k, "yso" + k]),
+                                              (1 - me, (1, 2, 7, 0), ["wf", "ath", "wlb", "lf", "ls0", "ycx" + k, "ysx" + k]))):
+            for b in range(4):
+                lb = ("mh%d" if i == 0 else "md%d") % b
+                mm(lb, deps, bank[bb[b]][:, 0:128], "qc", 384 + 128 * b, "yq" + k, 128 * half, 128 * half + 128)
+                yo = T.yt[:, 512 * half + b:512 * half + 512:4]
+                if b == 1 or (i == 0 and b == 3):
+                    act("ys", [lb], yo, bank[bb[b]][:, 0:128])
+                else:
+                    do("v", "yv", [lb], V.tensor_copy, yo, bank[bb[b]][:, 0:128])
+        step = (2, 3)[t]
+        n = C // step
+        for c in range(step):
+            do("v", "xn%d" % c, ["yv", "ys", "off"], V.tensor_tensor, xn[:, 4 * n * c:4 * n * (c + 1)],
+               T.yt[:, 0:1024].indirect(T.off[:, n // 4 * c:n // 4 * (c + 1)]), x[:, 4 * n * c:4 * n * (c + 1)], ALU.add)
+            for e in ([c] if t == 0 else [[], [0], [1, 2]][c]):
+                quant(("qx%d", "qy%d")[t] % e, ["xn%d" % e], "qx%d" % (t + 1), n * e, n * (e + 1), "x%d" % (t + 1), 4 * n * e)
+
+    for c in range(3):
+        a, b = 128 * c, 128 * c + 128
+        mm("my%d" % c, ["qy%d" % c, "vq"], bank[3 + c][:, 0:128], "vq", 0, "qx2", a, b)
+        if c < 2:
+            act("yo%d" % c, ["my%d" % c], T.yo[:, a:b], bank[3 + c][:, 0:128])
+        else:
+            do("v", "yo%d" % c, ["my%d" % c], V.tensor_copy, T.yo[:, a:b], bank[3 + c][:, 0:128])
+        dma("q", "so", ["qy%d" % c], T.oc[:, 4 * a:4 * b], T.qx2[:, a:b].bitcast(dt.uint8))
+        dma("q", "so", ["yo%d" % c], T.y[:, a:b], T.yo[:, a:b])
+    for i in range(4):
+        dma("s", "ss", ["qy0", "qy1", "qy2"], T.osc[4 * i:4 * i + 4, :], T.qx2s[32 * i:32 * i + 4, :])
+    w("s", "ss")
+    for lb in list(cnt):
+        if done.get(lb, 0) < cnt[lb]:
+            w("g" if lb == "lr" else "q", lb)

@@ -4,7 +4,11 @@ from concourse.mybir import dt, AluOpType, ActivationFunctionType, AxisListType
 ALU, ACT = AluOpType, ActivationFunctionType
 NR = 8
 C = 384
-BIG = 2.0 ** 30
+NS = 192
+OWN = 48
+L0 = NS - OWN
+LAND = L0 + NR * NS
+STEP = 512.0
 
 
 def _scratch():
@@ -22,29 +26,28 @@ def _scratch():
     bf("ut", 512); bf("vt", 512)
     for t in range(3):
         bf("x%d" % t, 4 * C); mx("qx%d" % t, C)
-    bf("ab", 4 * C); bf("hc", 1024); bf("zt", 512); bf("z", 1024); bf("ht", 512); bf("pr", 512)
-    bf("ct", 3584); bf("yt", 1024); bf("pf", C); bf("wf", C); bf("sj", 2 * C); bf("wzi", 512)
-    f32("pth", C); f32("ath", C); f32("s15", C); f32("mk", 2 * C); f32("ix", 2); f32("fc", 64); f32("m8", 8); f32("ni", 8)
-    f32("lf", 96); f32("yo", C); f32("wlb", C); f32("mi", 128); f32("fi", 512); f32("gw", 512); f32("et", 1024)
-    f32("wn", 32); f32("wt", 128); f32("wm", 32); f32("wi", 32); f32("la", 24)
-    i32("ic", 16); i32("jc", 16); i32("mj", 128); i32("lu", 16); i32("ai", 16); i32("dg", 64)
-    u16("lup", 24); u16("lua", 16); u16("ls", 16); u16("off", 96)
-    mx("uq", 128); mx("up", 384); mx("ua", 256); mx("vq", 128); mx("wq", 512); mx("qab", C); mx("qhc", 256); mx("zq", 128)
-    mx("qz", 256); mx("qpr", 128); mx("qc", 896)
+    bf("fl", 4 * C); bf("hc", 1024); bf("z", 224 + 512); bf("ht", 4 * (C + 2)); bf("pr", 512); bf("ct", 4096); bf("yt", 4 * NS + 16)
+    bf("wzi", 256); bf("seg", NS); bf("dm", NS)
+    f32("thr", C); f32("sr", C + 2); f32("sc", 2 * C); f32("fc", 96); f32("ni", 32); f32("zm", 56); f32("stc", 2)
+    f32("yo", C); f32("wlb", C); f32("mi", 128); f32("fi", 516); f32("gw", 512); f32("et", 1040)
+    f32("sg", 2 * NS); f32("wn", 64); f32("la", 8); f32("tw", 24)
+    i32("jc", 24); i32("mj", 128); i32("lu", 8); i32("ai", 56); i32("dg", 224)
+    u16("lup", 16); u16("ls", 12); u16("off", 96); u16("tl", 4)
+    mx("uq", 128); mx("up", 256); mx("vq", 128); mx("wq", 512); mx("qfl", C); mx("qhc", 256)
+    mx("qz", 128); mx("qpr", 128); mx("qc", 1024); mx("qh", C + 2)
     for t in range(2):
         k = str(t)
-        f32("rm" + k, 2 * C); f32("stl" + k, 32); f32("rst" + k, 1); u16("tl" + k, 2)
-        mx("ca" + k, 128); mx("cb" + k, 128); mx("land" + k, 288); mx("tq" + k, 128); mx("qh" + k, 128); mx("yq" + k, 256)
-        mx("rp" + k, 64); mx("ry" + k, 32)
+        f32("so" + k, 12); f32("stl" + k, 32); f32("rst" + k, 6)
+        mx("land" + k, LAND); mx("yq" + k, NS); mx("rp" + k, 2 * OWN)
     for b in range(8):
         s["b%d" % b] = ("psum", [128, 512], "float32")
     return s
 
 
 SCRATCH = _scratch()
-_REMOTE = ["st", "pc", "ps", "yco", "yso", "ycx", "ysx"]
+_REMOTE = ["st", "pc", "ps", "yc", "ys"]
 _RSEMS = [n + str(t) for t in range(2) for n in _REMOTE] + ["lr"]
-SEMAPHORES = _RSEMS + ["c%d" % i for i in range(135)]
+SEMAPHORES = _RSEMS + ["c%d" % i for i in range(139)]
 
 
 def _m(engines):
@@ -62,8 +65,7 @@ def _plan(T, topo):
         can = [c for c in topo.cores_of(cs[r]) if c != cs[r] and all(topo.may_write(c, cs[d]) for d in cross[r])]
         near = [c for c in can if topo.die(c) == topo.die(cs[r])]
         far = [c for c in can if topo.die(c) != topo.die(cs[r])]
-        a, b = (near, far) if kk[r] % 2 == 0 else (far, near)
-        relay.append([(a[0], 0, 0), (b[0], 2, 0), (a[1], 0, 1), (b[1], 2, 1)])
+        relay.append([(far[0], 0, 0), (far[1], 2, 0), (near[0], 0, 1), (near[1], 2, 1)])
     return cs, par, own, cross, kk, relay
 
 
@@ -72,45 +74,38 @@ def _dst(topo, d, core):
     return DstId(rid=rid, pnc=pid)
 
 
-def _direct(topo, r, d, cs, own):
-    o = [s for s in own[r] if s != r]
+def _direct(topo, r, d, cs, own, kind):
+    i = (own[r].index(d) - own[r].index(r)) % 4 - 1
     e = topo.engines(cs[r], cs[d])
-    i = o.index(d)
-    return (e[0:4], e[4:6], e[6:8])[i], (e[0:2], e[2:4], e[4:8])[i]
+    return ((e[0:4], e[4:6], e[6:8]), (e[0:2], e[4:8], e[2:4]), (e[0:2], e[2:4], e[4:8]))[kind][i]
+
+
+def _u8(T, name, what, a, b):
+    v = T[name + what][:, a:b]
+    return v if what else v.bitcast(dt.uint8)
 
 
 def _relay_program(g, core, T, topo, r, first, role, plan):
     cs, par, own, cross, kk, relay = plan
-    d0, d1 = cross[r][first], cross[r][first + 1]
-    eng = topo.engines(core, cs[d0])
-    ids = [_dst(topo, cs[d], core) for d in (d0, d1)]
-    loc = [0]
-    what = "s" if role else ""
-
-    def u8(v):
-        return v if role else v.bitcast(dt.uint8)
-
-    def send(trs, n):
-        g.remote_dma_fused(trs, local_sem=T.sem.lr)
-        loc[0] += n
-
+    ids = [_dst(topo, cs[d], core) for d in cross[r][first:first + 2]]
+    eng = topo.engines(core, cs[cross[r][first]])
+    half = [eng[0:4], eng[4:8]]
+    n, a = 0, L0 + NS * r
     for t in range(2):
         k = str(t)
-        sm = T.sem["st" + k]
-        g.wait_ge(sm, 8)
-        send([RemoteDMATransfer(dst_ids=[ids[role]], dma_engine_mask=_m(eng), remote_sem=sm, srcs=[T["rst" + k][:]], dsts=[T["stl" + k][:, 4 * r:4 * r + 1]])], len(eng))
-        sm = T.sem[("ps" if role else "pc") + k]
-        g.wait_ge(sm, 8)
-        half = [eng[0:4], eng[4:8]]
-        send([RemoteDMATransfer(dst_ids=[ids[i]], dma_engine_mask=_m(half[i]), remote_sem=sm, srcs=[u8(T["rp" + k + what][:, 32 * i:32 * i + 32])],
-                                dsts=[u8(T["land" + k + what][:, 32 * r:32 * r + 32])]) for i in range(2)], len(eng))
-        a = 128 * par[r] + 32 * kk[r]
-        sm = T.sem[("ysx" if role else "ycx") + k]
-        g.wait_ge(sm, 8 if role else 16)
-        d = T["yq" + k + what]
-        send([RemoteDMATransfer(dst_ids=ids, dma_engine_mask=_m(eng), remote_sem=sm, srcs=[u8(T["ry" + k + what][:, 0:32])],
-                                dsts=[u8(d[:, a:a + 32]), u8(d[:, a:a + 32])])], len(eng))
-    g.wait_ge(T.sem.lr, loc[0])
+        for kind in (("s",) if role else ("t", "")):
+            sm = T.sem[{"": "pc", "s": "ps", "t": "st"}[kind] + k]
+            g.wait_ge(sm, 4)
+            trs = []
+            for i in range(2):
+                if kind == "t":
+                    src, dst = T["rst" + k][:, 3 * i:3 * i + 3], T["stl" + k][:, 4 * r:4 * r + 3]
+                else:
+                    src, dst = _u8(T, "rp" + k, kind, OWN * i, OWN * i + OWN), _u8(T, "land" + k, kind, a, a + OWN)
+                trs.append(RemoteDMATransfer(dst_ids=[ids[i]], dma_engine_mask=_m(half[i]), remote_sem=sm, srcs=[src], dsts=[dst]))
+            g.remote_dma_fused(trs, local_sem=T.sem.lr)
+            n += len(eng)
+    g.wait_ge(T.sem.lr, n)
 
 
 def rank_program(g, core, T, topo):
@@ -127,10 +122,10 @@ def rank_program(g, core, T, topo):
 
 def _rank_program(g, core, T, topo, r, plan):
     cs, par, own, cross, kk, relay = plan
-    me, mk = par[r], kk[r]
-    peers = [s for s in own[r] if s != r]
+    mk = kk[r]
+    peers = [own[r][(mk + i) % 4] for i in (1, 2, 3)]
     V, S, P = g.vector, g.scalar, g.tensor
-    names, cnt, seen, done = {}, {}, {}, {}
+    names, cnt, seen, done, cols = {}, {}, {}, {}, {}
     bank = [T["b%d" % i] for i in range(8)]
     qid = {"g": g, "v": V, "s": S, "p": P, "q": g.sync}
 
@@ -164,27 +159,42 @@ def _rank_program(g, core, T, topo, r, plan):
         else:
             do("v", label, deps, V.tensor_scalar, out, in0, s1, s2, op0, op1)
 
-    def mm(label, deps, out, lhs, la, rhs, ra, rb):
-        do("p", label, deps, P.matmul_mx, out, T[lhs][:, la:la + 128], T[lhs + "s"][:, la:la + 128], T[rhs][:, ra:rb], T[rhs + "s"][:, ra:rb], True, True)
+    def tt(label, deps, out, in0, in1, op):
+        do("v", label, deps, V.tensor_tensor, out, in0, in1, op)
+
+    def cp(label, deps, out, in_):
+        do("v", label, deps, V.tensor_copy, out, in_)
+
+    def fill(label, out, c):
+        do("v", label, [], V.memset, out, c)
+
+    def mm(label, deps, b, lhs, la, rhs, ra, rb):
+        do("p", label, deps, P.matmul_mx, bank[b][:, 0:rb - ra], T[lhs][:, la:la + 128], T[lhs + "s"][:, la:la + 128], T[rhs][:, ra:rb], T[rhs + "s"][:, ra:rb], True, True)
 
     def quant(label, deps, out, a, b, tile, ta):
         do("v", label, deps, V.quantize_mx, T[out][:, a:b], T[out + "s"][:, a:b], T[tile][:, ta:ta + 4 * (b - a)])
 
-    def pick(label, deps, out, a, b, win, wa, wb, off, e, f):
-        do("v", label + "c", deps, V.tensor_copy, T[out][:, a:b].bitcast(dt.uint32), T[win][:, wa:wb].bitcast(dt.uint32).indirect(T[off][:, e:f]))
-        do("s", label + "s", deps, S.activation, T[out + "s"][:, a:b], T[win + "s"][:, wa:wb].indirect(T[off][:, e:f]), ACT.Copy)
+    def pickc(label, deps, out, a, b, win, wb, off, e, f):
+        cp(label + "c", deps, T[out][:, a:b].bitcast(dt.uint32), T[win][:, 0:wb].bitcast(dt.uint32).indirect(T[off][:, e:f]))
+
+    def picks(label, deps, out, a, b, win, wb, off, e, f):
+        do("s", label + "s", deps, S.activation, T[out + "s"][:, a:b], T[win + "s"][:, 0:wb].indirect(T[off][:, e:f]), ACT.Copy)
+
+    def pick(*a):
+        pickc(*a)
+        picks(*a)
 
     def act(label, deps, out, in_, func=ACT.Copy, **kw):
         do("s", label, deps, S.activation, out, in_, func, **kw)
 
-    def send(masks, deps, trs):
+    def send(deps, sm, trs):
         w("g", *deps)
-        g.remote_dma_fused(trs, local_sem=T.sem.lr)
-        cnt["lr"] = cnt.get("lr", 0) + sum(bin(m).count("1") for m in masks)
+        g.remote_dma_fused([RemoteDMATransfer(dst_ids=ids, dma_engine_mask=_m(e), remote_sem=T.sem[sm], srcs=[src], dsts=[dst for i in ids])
+                            for ids, e, src, dst in trs], local_sem=T.sem.lr)
+        cnt["lr"] = cnt.get("lr", 0) + sum(len(e) for ids, e, src, dst in trs)
 
     def u8(name, what, a, b):
-        v = T[name + what][:, a:b]
-        return v if what else v.bitcast(dt.uint8)
+        return _u8(T, name, what, a, b)
 
     def iota(label, out, pattern, base, ch, whole=False):
         if whole:
@@ -194,349 +204,337 @@ def _rank_program(g, core, T, topo, r, plan):
 
     fc = T.fc
 
-    def F(a, n=1):
-        return fc[:, a:a + n]
+    def F(name, n=1):
+        if name not in cols:
+            cols[name] = 16 + len(cols)
+        return fc[:, cols[name]:cols[name] + n]
+
+    def bit(j):
+        return fc[:, 7 - j:8 - j]
+
+    pv2, pv1, pv0, r0, p15, grp, kb = [fc[:, 8 + i:9 + i] for i in range(7)]
 
     dma("q", "Lu", [], T.ut[:], T.u[:])
-    dma("s", "Lx0", [], T.x0[:, 0:768], T.x[:, 0:768])
-    dma("q", "Lx1", [], T.x0[:, 768:1536], T.x[:, 768:1536])
-    dma("q", "Lw", ["Lx0", "Lx1"], T.wqs[:], T.ws[:])
+    dma("s", "Lx0", [], T.x0[:, 0:512], T.x[:, 0:512])
+    dma("q", "Lx1", [], T.x0[:, 512:1024], T.x[:, 512:1024])
+    dma("s", "Lx2", [], T.x0[:, 1024:1536], T.x[:, 1024:1536])
+    dma("q", "Lw", ["Lu"], T.wqs[:], T.ws[:])
     dma("q", "Lw", [], T.wq[:].bitcast(dt.uint8), T.wc[:])
-    dma("q", "Lv", [], T.vt[:], T.v[:])
+    dma("q", "Lv", ["Lw"], T.vt[:], T.v[:])
 
-    iota("gl", T.lu[:], [[1, 2], [0, 8]], 0, 16, True)
-    iota("gp", T.ic[:], [[0, 16]], 0, 1, True)
+    iota("gp", T.tw[:, 16:17], [[0, 1]], 0, 1)
+    iota("gp", T.tw[:, 0:16], [[-2, 2], [0, 8]], 2, 0)
+    iota("gl", T.lu[:], [[16, 8]], 1, 0, True)
     iota("gm", T.mi[:], [[1, 128]], 0, 0)
-    iota("gn", T.ni[:], [[1, 8]], 0, 0)
-    iota("gz", T.wzi[:], [[0, 8], [1, 16], [0, 4]], 0, 0)
-    iota("kz", T.z[:], [[0, 1024]], 0, 0)
-    iota("gf", T.fi[:], [[1, 512]], 0, 0)
-    iota("gf", T.wi[:], [[1, 16], [0, 2]], 0, 0)
-    iota("gf", T.gw[:], [[1, 32], [0, 4], [-1, 4]], 0, 0)
+    iota("gz", T.wzi[:], [[0, 4], [1, 16], [0, 4]], 0, 0)
+    iota("gn", T.ni[:, 0:18], [[0, 3], [1, 6]], 0, 0)
+    iota("gn", T.ni[:, 24:32], [[1, 8]], 0, 0)
+    one = T.z[:, 224:736]
+    iota("go", one, [[0, 512]], 1, 0)
+    iota("g0", T.z[:, 0:224], [[0, 224]], 0, 0)
+    iota("g0", T.ht[:, 0:8], [[0, 8]], 0, 0)
+    iota("gd", T.sg[:, 0:NS], [[0, 12], [1, 16]], 0, 0)
+    do("g", "gs", ["go"], g.affine_select, T.seg[:], T.z[:, 224:224 + NS], [[0, 12], [1, 16]], ALU.not_equal, 0.0, 0, 0)
+    pa = T.ct[:, 3587:4096:4]
+    do("g", "ga", [], g.affine_select, T.ct[:, 3584:4096], one, [[16, 8], [1, 16], [200, 4]], ALU.is_equal, 0.0, 2 - 600, -1)
+    do("g", "ga", ["ga"], g.affine_select, pa, pa, [[1, 8], [-1, 16]], ALU.not_equal, 0.0, 0, 0)
+    do("g", "ga", ["ga"], g.affine_select, pa, pa, [[0, 16], [16, 8]], ALU.not_equal, 1.0, 0, -1)
+    iota("gf", T.fi[:], [[1, 516]], -3, -4)
+    iota("gc", T.pr[:, C:512], [[0, 512 - C]], 0, 0)
+    iota("gc", T.yt[:, 0:4], [[0, 4]], 0, 0)
+    n8 = T.ni[:, 24:32]
 
-    do("v", "kzt", [], V.memset, T.zt[:], 0.0)
-    for i in range(2):
-        act("khm", ["kzt"], T.hc[:, 512 * i:512 * i + 512], T.zt[:])
-    for i in range(2):
-        act("kab", [], T.ab[:, 512 * i:512 * i + 512], T.zt[:])
-    do("v", "kl", [], V.memset, T.lup[:, 16:24], 15)
-    ts("kl", ["gl"], T.lu[:], T.lu[:], 113, ALU.bitwise_and)
-    do("v", "kl", ["kl"], V.tensor_copy, T.lup[:, 0:16], T.lu[:])
+    fill("khc", T.hc[:], -STEP)
+    fill("kl", T.lup[:, 0:8], 15)
+    do("v", "k0", ["gp"], V.tensor_tensor_scan, T.la[:, 0:8], T.tw[:, 0:8], T.tw[:, 8:16], T.tw[:, 16:17], ALU.mult, ALU.add)
+    cp("kl", ["gl"], T.lup[:, 8:16], T.lu[:])
+    cp("k0", ["k0"], T.jc[:, 16:24], T.la[:, 0:8])
+    w("v", "k0")
+    for a, b, sel, mask in ((0, 8, slice(16, 24), 256), (8, 11, slice(18, 23, 2), 384), (11, 13, slice(18, 21, 2), 480), (13, 15, slice(16, 21, 4), 224)):
+        ts("k0", [], T.jc[:, a:b], T.jc[:, sel], mask, ALU.bitwise_and)
+    w("v", "k0")
+    for a, b, d in ((0, 8, 256.0), (8, 11, 128.0), (11, 15, 32.0)):
+        ts("k0", [], fc[:, a:b], T.jc[:, a:b], 1.0 / d, ALU.mult)
+    ts("k3", ["k0"], F("r1"), pv2, 4.0, ALU.mult, pv0, ALU.add)
+    ts("k1", [], F("a0"), bit(4), -1.0, ALU.mult, 2.0, ALU.add)
+    ts("k1", [], F("a1"), bit(5), -3.0, ALU.mult, 4.0, ALU.add)
+    ts("k1", [], F("a2"), bit(6), -15.0, ALU.mult, 16.0, ALU.add)
+    ts("k1", [], F("p0"), p15, 0.0, ALU.is_equal)
+    ts("k1", [], F("g7"), T.tw[:, 16:17], 112.0, ALU.is_equal, 128.0, ALU.mult)
+    ts("k1", ["k1"], F("ak"), F("a0"), F("a1"), ALU.mult, F("a2"), ALU.mult)
 
-    def jbits(*specs):
-        for col, shift, mask in specs:
-            out, in0 = T.jc[:, col:col + 1], T.ic[:, 0:1]
-            if shift and mask:
-                ts("kj", ["gp"], out, in0, shift, ALU.logical_shift_right, mask, ALU.bitwise_and)
-            elif shift:
-                ts("kj", ["gp"], out, in0, shift, ALU.logical_shift_right)
-            else:
-                ts("kj", ["gp"], out, in0, mask, ALU.bitwise_and)
+    def equal(label, deps, out, in_, tmp, col):
+        act(label + "a", deps, tmp, in_, ACT.Abs, bias=col, scale=-1.0)
+        return lambda: act(label, [label + "a"], out, tmp, ACT.Relu, bias=1.0, scale=-1.0)
 
-    jbits((0, 0, 7), (2, 0, 1), (4, 1, 1), (6, 2, 1), (9, 5, 0), (10, 1, 15))
-    do("v", "kf", ["kj"], V.tensor_copy, fc[:, 0:8:2], T.jc[:, 0:8:2])
-    do("v", "kf", [], V.tensor_copy, fc[:, 9:11], T.jc[:, 9:11])
-    ts("k1", ["kf"], F(24), F(2), -1.0, ALU.mult, 2.0, ALU.add)
-    ts("k1", [], F(25), F(4), -3.0, ALU.mult, 4.0, ALU.add)
-    ts("k1", [], F(26), F(6), -15.0, ALU.mult, 16.0, ALU.add)
-    ts("k1", [], F(29), F(9), 2.0, ALU.mult, F(2), ALU.add)
-    ts("k1", [], F(23), F(0), 7.0, ALU.is_equal, 128.0, ALU.mult)
-    ts("k1", [], F(57), F(10), -1.0, ALU.mult)
-    ts("k1", ["k1"], F(27), F(24), F(25), ALU.mult, F(26), ALU.mult)
-    ts("k1", ["k1", "gm"], T.mj[:], T.mi[:], F(27), ALU.mult)
-    ts("k1", ["k1"], T.mj[:], T.mj[:], 128, ALU.bitwise_and)
-    w("v", "k1", "khm")
-    for h in range(2):
-        out = T.hc[:, 512 * h:512 * h + 512:4]
-        if (me if h else 1 - me):
-            ts("k1", [], out, T.mj[:], F(23), ALU.add, -BIG / 128, ALU.mult)
-        else:
-            ts("k1", [], out, T.mj[:], -BIG / 128, ALU.mult)
+    second = [equal("ky", ["gz", "k0"], T.ct[:, 256:512], T.wzi[:], T.et[:, 256:512], p15),
+              equal("ky", [], T.ct[:, 0:128], T.wzi[:, 0:128], T.et[:, 0:128], r0),
+              equal("ky", ["k3"], T.ct[:, 128:256], T.wzi[:, 0:128], T.et[:, 128:256], F("r1"))]
+    for f in second:
+        f()
+
+    todo = []
+
+    def later(label, deps, *a):
+        todo.append(lambda: ts(label, deps, *a))
+
+    def gap(n=1):
+        for i in range(min(n, len(todo))):
+            todo.pop(0)()
+
+    F("t2"), F("t1"), F("t0")
+    later("k2", [], F("b6"), bit(6), -2.0, ALU.add)
+    later("k2", [], F("n6"), bit(6), -100.0, ALU.mult, 102.0, ALU.add)
+    later("k2", ["k2"], F("t2", 3), fc[:, 8:11], 2.0, ALU.mult, F("b6"), ALU.add)
+    later("k2", [], F("t3"), pv2, F("n6"), ALU.add)
+    later("kz", ["gn"], T.zm[:, 27:56:4], n8, grp, ALU.is_equal)
+    for q in range(3):
+        later("kz", ["k2"], T.zm[:, q:56:4], T.ni[:, 0:14], F("t%d" % q), ALU.is_equal)
+    later("kz", [], T.zm[:, 3:24:4], T.ni[:, 0:6], F("t3"), ALU.is_equal)
+    todo.append(lambda: fill("kh", T.sr[:, 0:2], -1e29))
+    later("kc", [], T.wn[:, 32:51:9], T.ni[:, 0:3], 16.0, ALU.mult, p15, ALU.add)
+    later("kg", [], F("g4"), grp, 4.0, ALU.mult)
+    later("kn", [], F("c0"), bit(0), 1.0, ALU.add)
+    later("kn", [], F("c1"), bit(1), 3.0, ALU.mult, 1.0, ALU.add)
+    later("kn", [], F("c2"), bit(2), 15.0, ALU.mult, 1.0, ALU.add)
+    later("kn", [], F("d"), kb, grp, ALU.subtract, bit(4), ALU.add)
+    later("kn", [], F("u"), grp, 6.0, ALU.is_ge, 1.0, ALU.add)
+    later("kn", [], F("ne"), kb, grp, ALU.not_equal)
+    later("kn", [], F("lo"), p15, 8.0, ALU.is_lt, 4.0, ALU.mult)
+    later("kn", [], F("k7"), kb, 7.0, ALU.is_equal, -64.0, ALU.mult)
+    later("kn", ["kn"], F("pw"), F("c0"), F("c1"), ALU.mult, F("c2"), ALU.mult)
+    later("kn", [], F("gt"), F("d"), 1.0, ALU.is_gt, 0.25, ALU.mult)
+    later("kn", [], F("u0"), F("u"), F("c0"), ALU.mult, 32.0, ALU.mult)
+    later("kn", [], F("a5"), F("u"), -2.0, ALU.add, F("k7"), ALU.mult)
+    later("kn", [], F("ub"), F("u"), bit(4), ALU.mult, 128.0, ALU.mult)
+    later("kn", ["kn"], F("fa"), F("d"), 0.0, ALU.is_lt, F("gt"), ALU.add)
+    later("kn", [], F("ob"), F("ub"), 4.0, ALU.add, pv0, ALU.add)
+    later("kn", ["kn"], F("a3"), F("fa"), F("pw"), ALU.mult, F("a5"), ALU.add)
+    later("kn", [], F("a4"), F("fa"), 0.0, ALU.is_equal, F("u0"), ALU.mult)
+    later("kn", [], F("wl"), F("ne"), F("pw"), ALU.mult, F("lo"), ALU.mult)
+    later("kn", ["kn"], F("w1"), F("a3"), F("a4"), ALU.add, 256.0, ALU.add)
+    later("kn", ["kn"], F("w2"), F("w1"), F("ne"), ALU.mult, 256.0, ALU.subtract)
+    later("kn", ["kn"], F("w3"), F("w2"), F("lo"), ALU.mult)
+
+    gap(2)
     quant("uq", ["Lu"], "uq", 0, 128, "ut", 0)
-    pick("up", ["uq", "kl"], "up", 0, 256, "uq", 0, 128, "lup", 0, 16)
-    quant("qx0", ["Lx0"], "qx0", 0, 192, "x0", 0)
-    quant("qx1", ["Lx1"], "qx0", 192, 384, "x0", 768)
-    act("kab", [], T.ab[:, 1024:1536], T.zt[:])
-    pick("u5", [], "up", 256, 384, "uq", 0, 128, "lup", 16, 24)
-    quant("qhc", ["k1"], "qhc", 0, 256, "hc", 0)
-    quant("zq", ["kzt"], "zq", 0, 128, "zt", 0)
-    for t in range(2):
-        for what in ("", "s"):
-            dma("q", "kland", ["zq"], u8("land%d" % t, what, 256, 288), u8("zq", what, 0, 32))
-            dma("q", "kland", ["zq"], u8("tq%d" % t, what, 32, 128), u8("zq", what, 32, 128))
+    ts("k1", ["k1", "gm"], T.mj[:], T.mi[:], F("ak"), ALU.mult, F("p0"), ALU.mult)
+    pick("up", ["uq", "kl"], "up", 0, 128, "uq", 128, "lup", 0, 8)
+    ts("k1", ["k1"], T.mj[:], T.mj[:], 128, ALU.bitwise_and)
+    for c in range(3):
+        quant("qx%d" % c, ["Lx%d" % c], "qx0", 128 * c, 128 * c + 128, "x0", 512 * c)
+    pick("uo", ["uq"], "up", 128, 256, "uq", 128, "lup", 8, 16)
+    ts("k1", ["k1", "khc"], T.hc[:, 3:512:4], T.mj[:], -16 * STEP, ALU.mult)
+    ts("k1", [], T.hc[:, 515:1024:4], T.mj[:], F("g7"), ALU.add, -16 * STEP, ALU.mult)
 
-    def consts_a():
-        jbits((1, 4, 0), (3, 4, 1), (5, 5, 1), (7, 6, 1), (8, 3, 1), (11, 0, 3), (12, 0, 127), (14, 0, 15))
-        do("v", "kf", ["kj"], V.tensor_copy, fc[:, 1:8:2], T.jc[:, 1:8:2])
-        do("v", "kf", [], V.tensor_copy, F(8), T.jc[:, 8:9])
-        do("v", "kf", [], V.tensor_copy, F(11, 2), T.jc[:, 11:13])
-        do("v", "kf", [], V.tensor_copy, F(22), T.jc[:, 14:15])
-        ts("km8", ["kf"], F(30), F(12), 4.0, ALU.mult)
-        ts("kc", [], F(31), F(2), 16.0, ALU.mult, F(10), ALU.add)
-        if me == 0 and mk == 0:
-            ts("kwt", [], F(15), F(12), 0.0, ALU.is_equal, 2.0 ** 81, ALU.mult)
-            ts("kc", ["kwt"], F(32), F(15), -2.0 ** 50, ALU.add)
-        else:
-            do("v", "kc", [], V.memset, F(32), -2.0 ** 50)
-        do("v", "kwt", [], V.memset, T.wt[:, 0:32], 0.0)
-        ts("kwt", ["gf"], T.wm[:], T.wi[:], F(22), ALU.is_equal)
+    def unpackers():
+        act("kea", ["gf"], T.et[:, 0:516], T.fi[:], ACT.Abs)
         for b in range(4):
-            ts("ke0", ["km8"], F((28, 43, 55, 56)[b]), F(30), -1.0, ALU.mult, -float(b), ALU.add)
-        do("v", "kht", [], V.memset, T.ht[:], 0.0)
-        do("v", "kht", [], V.memset, T.pr[:, 384:512], 0.0)
-        unpackers(2)
-        unpackers(3)
+            act("kes", ["kea"], T.ct[:, 1536 + 512 * b:2048 + 512 * b], T.et[:, 3 - b:515 - b], ACT.Relu, bias=1.0, scale=-1.0)
 
-    def unpackers(b, stage=2):
-        e = T.et[:, 512 * (b % 2):512 * (b % 2) + 512]
-        if stage != 1:
-            act("kes", ["ke0", "gf"], e, T.fi[:], ACT.Abs, bias=F((28, 43, 55, 56)[b]))
-        if stage:
-            act("kes", ["kes"], T.ct[:, 1536 + 512 * b:2048 + 512 * b], e, ACT.Relu, bias=1.0, scale=-1.0)
+    def weighted(label, deps, a, col):
+        equal(label, deps, T.ct[:, a:a + 512], T.gw[:], T.et[:, 520:1032], F("g4"))()
+        act(label, [label, "kn"], T.ct[:, a:a + 512], T.ct[:, a:a + 512], ACT.Identity, scale=col)
 
-    def consts_b1():
-        ts("kn", [], F(18, 2), F(2, 2), 1.0, ALU.add)
-        ts("kn", [], F(20, 2), F(4, 2), 3.0, ALU.mult, 1.0, ALU.add)
-        ts("kn", [], F(13), F(6), 15.0, ALU.mult, 1.0, ALU.add)
-        ts("kn", [], F(14), F(7), 15.0, ALU.mult, 1.0, ALU.add)
-        ts("kn", [], F(35, 2), F(0, 2), 5.0, ALU.is_ge, 0.5, ALU.mult)
-        ts("kn", [], F(37, 2), F(0, 2), 0.0, ALU.is_equal, 15.5, ALU.mult)
-        ts("kn", [], F(44), F(0), 2.0, ALU.add)
-        ts("kn", [], F(45), F(0), F(1), ALU.not_equal)
-        ts("kn", [], F(46), F(8), -1.0, ALU.mult, 1.0, ALU.add)
-        ts("kn", [], F(54), F(1), 4.0, ALU.mult)
-        ts("kn", [], T.la[:, 0:8], T.ni[:], 16.0, ALU.mult)
-
-    def consts_b2():
-        do("v", "kn", ["kn"], V.tensor_tensor, F(33, 2), F(18, 2), F(20, 2), ALU.mult)
-        ts("kn", [], F(39, 2), F(35, 2), 0.5, ALU.add)
-        ts("kn", [], F(58, 6), T.ni[:, 0:6], F(0), ALU.not_equal, F(44), ALU.mult)
-        ts("kn", [], T.wn[:, 30:32], T.ni[:, 6:8], F(0), ALU.not_equal, F(44), ALU.mult)
-        ts("kn", [], T.la[:, 16:24], T.la[:, 0:8], 1.0, ALU.add)
-
-    def consts_b3():
-        do("v", "kn", ["kn"], V.tensor_tensor, F(16, 2), F(33, 2), F(13, 2), ALU.mult)
-        do("v", "kn", [], V.tensor_tensor, T.la[:, 8:14], F(58, 6), T.la[:, 0:6], ALU.add)
-        do("v", "kn", [], V.tensor_tensor, T.la[:, 14:16], T.wn[:, 30:32], T.la[:, 6:8], ALU.add)
-        do("v", "kn", ["kn"], V.tensor_tensor, F(41, 2), F(39, 2), F(16, 2), ALU.mult)
-        ts("kn", [], F(51), F(45), F(16), ALU.mult, F(46), ALU.mult)
-        do("v", "kla", [], V.tensor_copy, T.lua[:], T.la[:, 8:24])
-        do("v", "kn", ["kn"], V.tensor_tensor, F(47, 2), F(41, 2), F(37, 2), ALU.add)
-        ts("kn", ["kn"], F(49), F(47), 4.0, ALU.mult, 1024.0, ALU.add)
-        ts("kn", [], F(50), F(48), 4.0, ALU.mult, F(11), ALU.add)
-        ts("kn", ["kn"], F(52), F(49), F(45), ALU.mult, 1024.0, ALU.subtract)
-        ts("kn", ["kn"], F(53), F(52), F(46), ALU.mult)
-
-    def consts_c():
-        pick("ua", ["kla"], "ua", 0, 256, "uq", 0, 128, "lua", 0, 16)
-        ts("kw", ["gf", "kn"], T.ct[:, 512:1024], T.gw[:], F(54), ALU.is_equal, F(53), ALU.mult)
-        quant("qwl", ["kw"], "qc", 128, 256, "ct", 512)
-
-    def consts_d():
-        ts("kv", [], T.ct[:, 1024:1536], T.fi[:], F(54), ALU.is_equal, F(51), ALU.mult)
-        quant("qww", ["kv"], "qc", 256, 384, "ct", 1024)
-        quant("vq", ["Lv"], "vq", 0, 128, "vt", 0)
-
-    codes_to, scales_to = relay[r][0:2], relay[r][2:4]
     e_off = topo.engines(core, cs[peers[0]])
-    e_on = [e for e in topo.engines(core, codes_to[0][0]) if e not in e_off]
-    rid = {"": [_dst(topo, c[0], core) for c in codes_to], "s": [_dst(topo, c[0], core) for c in scales_to]}
+    e_on = [e for e in topo.engines(core, relay[r][0][0]) if e not in e_off]
+    rid = [_dst(topo, c[0], core) for c in relay[r]]
     pid = [_dst(topo, cs[d], core) for d in peers]
+    mine = L0 + NS * r
+    c0 = mine - OWN * mk
+    fl, sr = T.fl, T.sr
 
     for t in range(2):
         k = str(t)
         qx, x, xn = "qx" + k, T["x" + k], T["x%d" % (t + 1)]
-        rm = T["rm" + k]
-        for i in range(2):
-            lo, hi = 192 * i, 192 * i + 192
-            mm("mpt%d" % i, ["qx%d" % i, "upc", "ups"], bank[(1, 4)[i]][:, 0:192], "up", 128, qx, lo, hi)
-            mm("mp%d" % i, [], bank[(0, 3)[i]][:, 0:192], "up", 0, qx, lo, hi)
-            act("pth%d" % i, ["mpt%d" % i], T.pth[:, lo:hi], bank[(1, 4)[i]][:, 0:192])
-        mm("ms", ["u5c", "u5s"], bank[2][:, 0:C], "up", 256, qx, 0, C)
-        act("s15", ["ms"], T.s15[:], bank[2][:, 0:C], scale=1.0 / BIG)
-        if t == 0:
-            act("kwz", ["gz", "k1"], T.et[:, 0:512], T.wzi[:], ACT.Abs, bias=F(57))
-            act("kwz", ["kwz"], T.ct[:, 0:512], T.et[:, 0:512], ACT.Relu, bias=1.0, scale=-1.0)
-        for i in range(2):
-            lo, hi = 192 * i, 192 * i + 192
-            do("v", "pf%d" % i, ["mp%d" % i, "pth%d" % i], V.tensor_tensor, T.pf[:, lo:hi], bank[(0, 3)[i]][:, 0:192], T.pth[:, lo:hi], ALU.is_le)
-            if i:
-                quant("qab", ["ab"], "qab", 0, 192, "ab", 0)
-            ts("ab", ["pf%d" % i, "kab"], T.ab[:, 4 * lo:4 * hi:4], T.pf[:, lo:hi], BIG, ALU.mult)
-        quant("qab", ["ab"], "qab", 192, 384, "ab", 768)
-        for h in range(2):
-            mm("mc%d" % h, ["qab", "qhc"], bank[5 + h][:, 0:C], "qhc", 128 * h, "qab", 0, C)
+        land, yq = "land" + k, "yq" + k
 
-        def scores():
-            mm("ma", ["uac", "uas", "pth0", "pth1"], bank[1][:, 0:C], "ua", 0, qx, 0, C)
-            mm("mat", ["s15"], bank[2][:, 0:C], "ua", 128, qx, 0, C)
+        def tr(c, b):
+            mm("mt%d" % c, ["qx%d" % c, "uq"], b, qx, 128 * c, "uq", 0, 128)
+
+        def sign(j, lo, hi, src, deps):
+            act("sg", ["stc"] + deps, fl[:, 4 * lo + j:4 * hi:4], src, ACT.Sign, bias=T.stc[:, j:j + 1], scale=-1.0)
+
+        def less(j, lo, hi, src, b, deps):
+            ts("ls%d" % j, deps, fl[:, 4 * lo + j:4 * hi:4], src, bank[b][:, 15:16], ALU.is_lt)
+
+        def layer(b, bk, deps, lo=0, hi=C):
+            mm("mh%d" % b, ["Lw"] + deps, bk, "wq", 128 * b, qx, lo, hi)
+            act("ht" if hi == C else "h0", ["mh%d" % b], T.ht[:, 8 + 4 * lo + b:8 + 4 * hi:4], bank[bk][:, 0:hi - lo], scale=0.03125)
 
         if t == 0:
-            ts("km8", ["gn"], T.m8[:], T.ni[:], F(29), ALU.is_equal)
-            do("v", "km8", [], V.memset, T.dg[:], 0)
+            tr(0, 0)
+            tr(1, 1)
+            tr(2, 2)
+            mm("ms0", ["upc", "ups"], 3, "up", 0, qx, 0, C)
+            mm("mth", ["uoc", "uos"], 4, "up", 128, qx, 0, C)
+            mm("ms1", [], 5, "up", 0, qx, 0, C)
+            mm("mp", [], 6, "uq", 0, qx, 0, C)
+            act("stc", ["mt0"], T.stc[:, 0:1], bank[0][:, 15:16])
+            less(1, 0, C, bank[3][:, 0:C], 1, ["ms0", "mt1"])
+            less(2, 0, C, bank[3][:, 0:C], 2, ["mt2"])
+            act("thr", ["mth"], T.thr[:], bank[4][:, 0:C])
+            sign(0, 0, C, bank[5][:, 0:C], ["ms1"])
+            act("sr", [], sr[:, 2:C + 2], bank[5][:, 0:C])
+            tt("pf", ["mp", "thr"], fl[:, 3:4 * C:4], bank[6][:, 0:C], T.thr[:], ALU.is_le)
+            quant("qhc", ["k1"], "qhc", 0, 256, "hc", 0)
+            layer(0, 7, ["stc"])
+            layer(1, 0, [])
+            kbk = (4, 5)
         else:
-            scores()
+            for c in range(3):
+                lo, hi = 128 * c, 128 * c + 128
+                w("p", "stc")
+                tr(c, 0)
+                mm("ms0", ["sr", "sg"], 1, "up", 0, qx, lo, hi)
+                mm("mth", ["thr"], 2, "up", 128, qx, lo, hi)
+                if c < 2:
+                    act("stc", ["mt%d" % c], T.stc[:, c:c + 1], bank[0][:, 15:16])
+                else:
+                    mm("mp", [], 7, "uq", 0, qx, 0, C)
+                    less(2, 0, lo, sr[:, 2:2 + lo], 0, ["sr", "mt2"])
+                act("sr", ["ms0"], sr[:, 2 + lo:2 + hi], bank[1][:, 0:128])
+                act("thr", ["mth"], T.thr[:, lo:hi], bank[2][:, 0:128])
+                for j in range(min(c + 1, 2)):
+                    sign(j, lo, hi, bank[1][:, 0:128], [])
+                if c == 1:
+                    sign(1, 0, lo, sr[:, 2:2 + lo], ["sr"])
+                if c != 1:
+                    w("p", "h0")
+                    for b in range(4):
+                        layer(b, 3 + b, [], 64 * c, hi)
+            tt("pf", ["mp", "thr"], fl[:, 3:4 * C:4], bank[7][:, 0:C], T.thr[:], ALU.is_le)
+            less(2, 256, C, sr[:, 258:C + 2], 0, ["sr"])
+            kbk = (1, 2)
+        quant("qfl", ["pf", "sg", "ls1", "ls2"], "qfl", 0, C, "fl", 0)
+        if t:
+            quant("qh", ["h0"], "qh", 0, 130, "ht", 0)
         for h in range(2):
-            hs = str(h)
-            mk_, rmh = T.mk[:, C * h:C * h + C], rm[:, C * h:C * h + C]
-            last, sj = rm[:, C * h + C - 1:C * h + C], T.sj[:, C * h:C * h + C]
-            do("v", "mk" + hs, ["mc" + hs, "s15"], V.tensor_tensor, mk_, bank[5 + h][:, 0:C], T.s15[:], ALU.add)
-            do("v", "rm" + hs, ["mk" + hs], V.tensor_tensor_scan, rmh, mk_, mk_, -1e29, ALU.max, ALU.max)
-            act("ix" + hs, ["rm" + hs], sj, rmh, ACT.Sign, bias=last, scale=-1.0, accum_out=T.ix[:, h:h + 1])
+            mm("mk%d" % h, ["qfl", "qhc", "sr"], kbk[h], "qhc", 128 * h, "qfl", 0, C)
         if t == 0:
-            quant("qwz", ["kwz"], "qc", 0, 128, "ct", 0)
-        else:
-            act("ath", ["mat"], T.ath[:], bank[2][:, 0:C])
-        send([_m(e_on)], ["rm0"], [RemoteDMATransfer(dst_ids=rid[""] + rid["s"], dma_engine_mask=_m(e_on), remote_sem=T.sem["st" + k],
-                                                     srcs=[rm[:, C - 1:C]], dsts=[T["rst" + k][:] for i in range(4)])])
-        send([_m(e_off)], ["rm1"], [RemoteDMATransfer(dst_ids=pid, dma_engine_mask=_m(e_off), remote_sem=T.sem["st" + k], srcs=[rm[:, 2 * C - 1:2 * C]],
-                                                      dsts=[T["stl" + k][:, 4 * r:4 * r + 1] for d in peers])])
-
-        def digits(h):
-            hs, ai = str(h), T.ai[:, 8 * h:8 * h + 8]
-            ts("da" + hs, ["ix" + hs, "km8"], ai, T.m8[:], T.ix[:, h:h + 1], ALU.mult)
-            for b, ma in enumerate((448, 56, 7)):
-                ts("db" + hs, ["da" + hs], T.dg[:, 32 * h + b:32 * h + 32:4], ai, ma, ALU.bitwise_and)
-
-        def spread(h):
-            hs = str(h)
-            do("v", "dz" + hs, ["db" + hs, "kz"], V.tensor_copy, T.z[:, 512 * h:512 * h + 32], T.dg[:, 32 * h:32 * h + 32])
-            quant("qz" + hs, ["dz" + hs], "qz", 128 * h, 128 * h + 128, "z", 512 * h)
-            mm("mz" + hs, ["qz" + hs, "qwz"], bank[(7, 0)[h]][:, 0:128], "qc", 0, "qz", 128 * h, 128 * h + 128)
-
-        def choose(h):
-            hs = str(h)
-            do("v", "ls" + hs, ["mz" + hs], V.tensor_copy, T.ls[:, 8 * h:8 * h + 8], bank[(7, 0)[h]][:, 0:8])
-            pick("c" + hs, ["ls" + hs], ("ca", "cb")[h] + k, 0, 128, qx, 0, C, "ls", 8 * h, 8 * h + 8)
-
-        digits(0)
-        spread(0)
-        digits(1)
-        choose(0)
-        spread(1)
-        choose(1)
-        for what, sm, lb in (("", "pc", "c0c"), ("s", "ps", "c0s")):
-            ms = [_m(e_on), _m(e_off)]
-            send(ms, [lb], [RemoteDMATransfer(dst_ids=[rid[what][i]], dma_engine_mask=ms[i], remote_sem=T.sem[sm + k],
-                                              srcs=[u8("ca" + k, what, 32 * codes_to[i][1], 32 * codes_to[i][1] + 64)], dsts=[u8("rp" + k, what, 0, 64)]) for i in range(2)])
-        for what, sm, lb in (("", "pc", "c1c"), ("s", "ps", "c1s")):
-            ms = [_m(_direct(topo, r, d, cs, own)[1 if what else 0]) for d in peers]
-            send(ms, [lb], [RemoteDMATransfer(dst_ids=[pid[i]], dma_engine_mask=ms[i], remote_sem=T.sem[sm + k],
-                                              srcs=[u8("cb" + k, what, 32 * kk[d], 32 * kk[d] + 32)], dsts=[u8("land" + k, what, 32 * r, 32 * r + 32)]) for i, d in enumerate(peers)])
-        for what, lb in (("", "c1c"), ("s", "c1s")):
-            dma("q", "cown" + what, [lb], u8("land" + k, what, 32 * r, 32 * r + 32), u8("cb" + k, what, 32 * mk, 32 * mk + 32))
-        do("v", "sown", ["rm1"], V.tensor_copy, T["stl" + k][:, 4 * r:4 * r + 1], rm[:, 2 * C - 1:2 * C])
-
-        def wishes():
-            do("v", "wf", ["ma", "ath"], V.tensor_tensor, T.wf[:], bank[1][:, 0:C], T.ath[:], ALU.is_gt)
-            do("v", "pr", ["wf", "kht"], V.tensor_tensor, T.pr[:, 0:C], T.wf[:], T.pf[:], ALU.is_gt)
+            layer(2, 1, [])
+            layer(3, 2, [])
+            equal("kd", ["gd"], T.dm[:], T.sg[:, 0:NS], T.et[:, 520:520 + NS], p15)()
+            gap(7)
+        for h, (a, b) in enumerate(((0, 24), (24, 56))):
+            do("v", "sc%d" % h, ["mk%d" % h, "go"], V.tensor_tensor_scan, T.sc[:, C * h:C * h + C], T.z[:, 224:224 + C], bank[kbk[h]][:, 0:C], -STEP * 1024, ALU.add, ALU.max)
+        for h, (a, b) in enumerate(((0, 24), (24, 56))):
+            ts("ai", ["sc%d" % h, "kz"], T.ai[:, a:b], T.zm[:, a:b], T.sc[:, C * h + C - 1:C * h + C], ALU.mult, 16.0, ALU.add)
+        if t == 0:
+            quant("qy", ["ky"], "qc", 0, 128, "ct", 0)
+        w("v", "ai", "g0")
+        for b, ma in enumerate((480, 31)):
+            ts("dg", [], T.dg[:, 56 * b:56 * b + 56], T.ai[:], ma, ALU.bitwise_and)
+        gap()
+        cp("dz", ["dg"], T.z[:, 0:224:4], T.dg[:, 0:56])
+        ts("dz", [], T.z[:, 1:224:4], T.dg[:, 56:112], -16.0, ALU.add)
+        gap()
+        quant("qz", ["dz"], "qz", 0, 128, "z", 0)
+        mm("mz", ["qz", "ht" if t else "qy"], 3, "qc", 0, "qz", 0, 128)
+        quant("qh", ["ht"], "qh", 130 * t, C + 2, "ht", 520 * t)
+        w("v", "mz")
+        for q in range(4):
+            src = bank[3][32 * q:32 * q + 32, q:48:4] if q < 3 else bank[3][96:128, 11:56:4]
+            ts("ls", [], T.ls[32 * q:32 * q + 32, :], src, -1.0, ALU.mult, float(C + 1), ALU.add)
+        picks("c", ["ls", "qh"], land, c0, c0 + NS, "qh", C + 2, "ls", 0, 12)
+        so, stl = T["so" + k], T["stl" + k]
+        gap()
+        tt("sa", ["ls", "sr", "kd", "kh"], T.sg[:, 0:NS], sr[:, 0:C + 2].indirect(T.ls[:, 0:12]), T.dm[:], ALU.mult)
+        gap()
+        do("v", "sb", ["sa", "gs"], V.tensor_tensor_scan, T.sg[:, NS:2 * NS], T.seg[:], T.sg[:, 0:NS], 0.0, ALU.mult, ALU.add)
+        gap()
+        cp("so", ["sb"], so[:], T.sg[:, NS + 15:2 * NS:16])
+        pickc("c", ["qh"], land, c0, c0 + NS, "qh", C + 2, "ls", 0, 12)
+        cp("sown", ["so"], stl[:, 4 * r:4 * r + 3], so[:, 3 * mk:3 * mk + 3])
+        for kind, (what, sm, lb) in enumerate((("s", "ps", "cs"), ("t", "st", "so"), ("", "pc", "cc"))):
+            def piece(o, n):
+                return so[:, 3 * o:3 * (o + n)] if what == "t" else u8(land, what, c0 + OWN * o, c0 + OWN * (o + n))
+            rl = (2, 3) if what == "s" else (0, 1)
+            send([lb], sm + k, [([rid[j]], e_on[4 * i:4 * i + 4], piece(relay[r][j][1], 2), T["rst" + k][:] if what == "t" else u8("rp" + k, what, 0, 2 * OWN))
+                                for i, j in enumerate(rl)])
+            send([], sm + k, [([pid[i]], _direct(topo, r, d, cs, own, kind), piece(kk[d], 1), stl[:, 4 * r:4 * r + 3] if what == "t" else u8(land, what, mine, mine + OWN))
+                              for i, d in enumerate(peers)])
+            cnt[sm + k] = sum(len(_direct(topo, s, r, cs, own, kind)) for s in peers) + 16
 
         def offsets():
-            quant("qpr", ["pr"], "qpr", 0, 128, "pr", 0)
-            mm("ml", ["qpr", "qwl", "ls1"], bank[0][:, 0:128], "qc", 128, "qpr", 0, 128)
-            ts("lf", ["ml"], T.lf[:], bank[0][:, 0:96], F(50), ALU.add)
-            do("v", "off", ["lf"], V.tensor_copy, T.off[:], T.lf[:])
+            mm("ml", ["qpr", "qwl"], 0, "qc", 128, "qpr", 0, 128)
+            ts("off", ["ml"], T.off[:], bank[0][:, 0:96], F("ob"), ALU.add)
 
         if t == 0:
-            consts_a()
-            consts_b1()
-        else:
-            wishes()
-        cnt["st" + k] = 8 * 3 + 8 * 4
-        wn, so = T.wn, T["stl" + k]
-        do("v", "w1", ["st" + k, "sown"], V.tensor_tensor_scan, wn[:, 0:8], so[:, 0:32:4], so[:, 0:32:4], -1e29, ALU.max, ALU.max)
-        ts("w1", ["w1"], wn[:, 8:16], wn[:, 0:8], wn[:, 7:8], ALU.is_lt, 32.0, ALU.mult)
-        ts("w1", ["kc"], wn[:, 18:19], wn[:, 7:8], F(32), ALU.is_lt, 256.0, ALU.mult)
-        do("v", "w1", ["w1"], V.tensor_reduce, wn[:, 16:17], wn[:, 8:16], AxisListType.X, ALU.add)
-        ts("w1", ["w1", "kwt"], T.wt[:, 0:1], wn[:, 16:17], F(31), ALU.add, wn[:, 18:19], ALU.max)
-        p0 = 32 * mk
-        do("v", "w2", ["w1"], V.transpose, T.wt[p0:p0 + 32, 32:64], T.wt[p0:p0 + 32, 0:32])
-        do("g", "w3", ["w2"], g.partition_broadcast, T.wt[:, 64:96], T.wt[p0:p0 + 1, 32:64], 128)
+            iota("gw", T.gw[:], [[1, 32], [0, 4], [-1, 4]], 0, 0)
+            quant("qpa", ["ga"], "qc", 896, 1024, "ct", 3584)
+            unpackers()
+        mm("ma", ["qpa", "ht"], 6, "qc", 896, "qfl", 0, C)
+        gap(6)
+        ts("pr", ["ma"], T.pr[:, 0:C], bank[6][:, 0:C], 0.0, ALU.is_equal)
+        gap(99)
         if t == 0:
-            consts_b2()
-        do("v", "w1", ["w3"], V.tensor_tensor, T.wt[:, 96:128], T.wt[:, 64:96], T.wm[:], ALU.mult)
-        for i in range(2):
-            do("v", "w4", ["w1"], V.tensor_reduce, wn[:, 20 + i:21 + i], T.wt[:, 96 + i:128:2], AxisListType.X, ALU.add)
-        do("v", "tl", ["w4"], V.tensor_copy, T["tl" + k][:], wn[:, 20:22])
-        cnt["pc" + k] = sum(len(_direct(topo, s, r, cs, own)[0]) for s in peers) + 16
-        cnt["ps" + k] = sum(len(_direct(topo, s, r, cs, own)[1]) for s in peers) + 16
-        win, tq = "land" + k, "tq" + k
-        w("v", "tl", "kland", "cown", "pc" + k)
-        w("s", "tl", "kland", "cowns", "ps" + k)
-        pick("t", [], tq, 0, 32, win, 0, 288, "tl" + k, 0, 2)
-        for b in range(4):
-            mm("mh%d" % b, ["tc", "ts", "Lw"], bank[3 + b][:, 0:128], "wq", 128 * b, tq, 0, 128)
-            if b != 1:
-                ts("hv", ["mh%d" % b, "kht"], T.ht[:, b:128:4], bank[3 + b][:, 0:32], 0.03125, ALU.mult)
-            else:
-                act("hs", ["mh%d" % b, "kht"], T.ht[:, b:128:4], bank[3 + b][:, 0:32], scale=0.03125)
-        qh = "qh" + k
-        quant("qh", ["hv", "hs"], qh, 0, 128, "ht", 0)
-        a = 128 * me + 32 * mk
-
-        def out(what, e):
-            return RemoteDMATransfer(dst_ids=rid[what], dma_engine_mask=_m(e), remote_sem=T.sem[("ysx" if what else "ycx") + k], srcs=[u8(qh, what, 0, 32)],
-                                     dsts=[u8("ry" + k, what, 0, 32) for i in range(2)])
-
-        def straight(what):
-            return RemoteDMATransfer(dst_ids=pid, dma_engine_mask=_m(e_off), remote_sem=T.sem[("yso" if what else "yco") + k], srcs=[u8(qh, what, 0, 32)],
-                                     dsts=[u8("yq" + k, what, a, a + 32) for d in peers])
-
-        send([_m(e_off + e_on)], ["qh"], [out("", e_off + e_on)])
-        send([_m(e_on), _m(e_off)], [], [out("s", e_on), straight("s")])
-        send([_m(e_off)], [], [straight("")])
-        for what in ("", "s"):
-            dma("q", "yown", ["qh"], u8("yq" + k, what, a, a + 32), u8(qh, what, 0, 32))
-        if t == 0:
-            consts_b3()
-            consts_c()
-            unpackers(0, 0)
-            scores()
-            act("ath", ["mat"], T.ath[:], bank[2][:, 0:C])
-            unpackers(0, 1)
-            unpackers(1)
-            wishes()
-            offsets()
+            weighted("kw", ["gw", "kg"], 512, F("w3"))
             quant("qe", ["kes"], "qc", 384, 896, "ct", 1536)
+            quant("qpr", ["pr", "gc"], "qpr", 0, 128, "pr", 0)
         else:
+            weighted("kv", ["gv"], 1024, F("wl"))
+            quant("qpr", ["pr"], "qpr", 0, 128, "pr", 0)
+            cp("pw", [], fl[:, 3:4 * C:4], T.pr[:, 0:C])
             offsets()
-            consts_d()
-            do("v", "pw", ["pr"], V.tensor_copy, T.ab[:, 0:4 * C:4], T.pr[:, 0:C])
-            quant("qpw", ["pw"], "qab", 0, C, "ab", 0)
-            mm("mw", ["qpw", "qww"], bank[7][:, 0:C], "qc", 256, "qab", 0, C)
-            ts("wlb", ["mw"], T.wlb[0:8, :], bank[7][0:8, 0:C], fc[0:8, 16:17], ALU.add)
-            dma("q", "so", ["wlb"], T.wl[:], T.wlb[0:8, :])
-        cnt["yco" + k] = cnt["yso" + k] = 24
-        cnt["ycx" + k] = cnt["ysx" + k] = 32
-        for i, (half, bb, deps) in enumerate(((me, (3, 4, 5, 6), ["qh", "qe", "yown", "yco" + k, "yso" + k]),
-                                              (1 - me, (1, 2, 7, 0), ["wf", "ath", "wlb", "lf", "ls0", "ycx" + k, "ysx" + k]))):
-            for b in range(4):
-                lb = ("mh%d" if i == 0 else "md%d") % b
-                mm(lb, deps, bank[bb[b]][:, 0:128], "qc", 384 + 128 * b, "yq" + k, 128 * half, 128 * half + 128)
-                yo = T.yt[:, 512 * half + b:512 * half + 512:4]
-                if b == 1 or (i == 0 and b == 3):
-                    act("ys", [lb], yo, bank[bb[b]][:, 0:128])
-                else:
-                    do("v", "yv", [lb], V.tensor_copy, yo, bank[bb[b]][:, 0:128])
-        step = (2, 3)[t]
-        n = C // step
-        for c in range(step):
-            do("v", "xn%d" % c, ["yv", "ys", "off"], V.tensor_tensor, xn[:, 4 * n * c:4 * n * (c + 1)],
-               T.yt[:, 0:1024].indirect(T.off[:, n // 4 * c:n // 4 * (c + 1)]), x[:, 4 * n * c:4 * n * (c + 1)], ALU.add)
-            for e in ([c] if t == 0 else [[], [0], [1, 2]][c]):
-                quant(("qx%d", "qy%d")[t] % e, ["xn%d" % e], "qx%d" % (t + 1), n * e, n * (e + 1), "x%d" % (t + 1), 4 * n * e)
+            quant("qpw", ["pw"], "qfl", 0, C, "fl", 0)
+        wn = T.wn
+        w("v", "st" + k, "sown", "kc")
+        for c in range(3):
+            do("v", "w1", [], V.tensor_tensor_scan, wn[:, 8 * c:8 * c + 8], stl[:, c:32:4], stl[:, c:32:4], -1e29, ALU.max, ALU.max)
+        w("v", "w1")
+        for c in range(3):
+            ts("w1", [], wn[:, 24 + 9 * c:32 + 9 * c], wn[:, 8 * c:8 * c + 8], wn[:, 8 * c + 7:8 * c + 8], ALU.is_lt, float(NS), ALU.mult)
+        w("v", "w1")
+        for c in range(3):
+            do("v", "w1", [], V.tensor_reduce, wn[:, 56 + c:57 + c], wn[:, 24 + 9 * c:33 + 9 * c], AxisListType.X, ALU.add)
+        ts("tl", ["w1"], T.tl[:, 0:3], wn[:, 56:59], float(L0), ALU.add)
+        a = OWN * mk
+        pickc("t", ["tl", "cc", "pc" + k], yq, a, a + OWN, land, LAND, "tl", 0, 3)
+        picks("t", ["tl", "cs", "ps" + k], yq, a, a + OWN, land, LAND, "tl", 0, 3)
+        for what, sm, lb in (("", "yc", "tc"), ("s", "ys", "ts")):
+            send([lb], sm + k, [(pid, e_off, u8(yq, what, a, a + OWN), u8(yq, what, a, a + OWN))])
+            cnt[sm + k] = 3 * len(e_off)
+        if t == 0:
+            quant("qwl", ["kw"], "qc", 128, 256, "ct", 512)
+            offsets()
+            quant("vq", ["Lv"], "vq", 0, 128, "vt", 0)
+            iota("gv", T.gw[:], [[1, 512]], -3, 0)
+        else:
+            quant("qww", ["kv"], "qc", 256, 384, "ct", 1024)
+            mm("mw", ["qpw", "qww", "ls"], 3, "qc", 256, "qfl", 0, C)
+            act("wlb", ["mw"], T.wlb[0:8, :], bank[3][0:8, 0:C], ACT.Identity, bias=fc[0:8, cols["pw"]:cols["pw"] + 1], scale=0.25)
+            dma("q", "so_", ["wlb"], T.wl[:], T.wlb[0:8, :])
+        for b, bk in enumerate((1, 2, 4, 5)):
+            mm("md%d" % b, ["qe", "tc", "ts", "yc" + k, "ys" + k], bk, "qc", 384 + 128 * b, yq, 0, NS)
+            yo = T.yt[:, 4 + b:4 + 4 * NS:4]
+            if b % 2 == 0:
+                act("ya", ["md%d" % b], yo, bank[bk][:, 0:NS])
+            else:
+                cp("yv", ["md%d" % b], yo, bank[bk][:, 0:NS])
+
+        def add(lb, a, b):
+            tt(lb, ["yv", "ya", "off"], xn[:, 16 * a:16 * b], T.yt[:, 0:4 * NS + 4].indirect(T.off[:, a:b]), x[:, 16 * a:16 * b], ALU.add)
+
+        add("xn0", 0, 32)
+        for c in range(3):
+            if c < 2:
+                add("xn%d" % (c + 1), 32 * c + 32, 32 * c + 40)
+            quant("qx%d" % c, ["xn%d" % c], "qx%d" % (t + 1), 128 * c, 128 * c + 128, "x%d" % (t + 1), 512 * c)
+            if c < 2:
+                add("xn%d" % (c + 1), 32 * c + 40, 32 * c + 64)
 
     for c in range(3):
         a, b = 128 * c, 128 * c + 128
-        mm("my%d" % c, ["qy%d" % c, "vq"], bank[3 + c][:, 0:128], "vq", 0, "qx2", a, b)
+        mm("my%d" % c, ["qx%d" % c, "vq"], 5 + c, "vq", 0, "qx2", a, b)
         if c < 2:
-            act("yo%d" % c, ["my%d" % c], T.yo[:, a:b], bank[3 + c][:, 0:128])
+            act("yo%d" % c, ["my%d" % c], T.yo[:, a:b], bank[5 + c][:, 0:128])
         else:
-            do("v", "yo%d" % c, ["my%d" % c], V.tensor_copy, T.yo[:, a:b], bank[3 + c][:, 0:128])
-        dma("q", "so", ["qy%d" % c], T.oc[:, 4 * a:4 * b], T.qx2[:, a:b].bitcast(dt.uint8))
-        dma("q", "so", ["yo%d" % c], T.y[:, a:b], T.yo[:, a:b])
+            cp("yo%d" % c, ["my%d" % c], T.yo[:, a:b], bank[5 + c][:, 0:128])
+        dma("q", "so_", ["qx%d" % c], T.oc[:, 4 * a:4 * b], T.qx2[:, a:b].bitcast(dt.uint8))
+        dma("q", "so_", ["yo%d" % c], T.y[:, a:b], T.yo[:, a:b])
     for i in range(4):
-        dma("s", "ss", ["qy0", "qy1", "qy2"], T.osc[4 * i:4 * i + 4, :], T.qx2s[32 * i:32 * i + 4, :])
+        dma("s", "ss", ["qx0", "qx1", "qx2"], T.osc[4 * i:4 * i + 4, :], T.qx2s[32 * i:32 * i + 4, :])
     w("s", "ss")
     for lb in list(cnt):
         if done.get(lb, 0) < cnt[lb]:

@@ -6,7 +6,7 @@ NR = 8
 C = 384
 NS = 192
 OWN = 48
-L0 = NS - OWN
+L0 = 160
 LAND = L0 + NR * NS
 STEP = 512.0
 
@@ -26,8 +26,8 @@ def _scratch():
     bf("ut", 512); bf("vt", 512)
     for t in range(3):
         bf("x%d" % t, 4 * C); mx("qx%d" % t, C)
-    bf("fl", 4 * C); bf("hc", 1024); bf("z", 224 + 512); bf("ht", 4 * (C + 2)); bf("pr", 512); bf("ct", 4096); bf("yt", 4 * NS + 16)
-    bf("wzi", 256); bf("seg", NS); bf("dm", NS)
+    bf("fl", 4 * C); bf("hc", 1024); bf("z", 224 + 512); bf("ht", 4 * (C + 2)); bf("pr", C + 256); bf("ct", 4096); bf("yt", 4 * NS + 16)
+    bf("hv", 256); bf("seg", NS); bf("dm", NS)
     f32("thr", C); f32("sr", C + 2); f32("sc", 2 * C); f32("fc", 96); f32("ni", 32); f32("zm", 56); f32("stc", 2)
     f32("yo", C); f32("wlb", C); f32("mi", 128); f32("fi", 516); f32("gw", 512); f32("et", 1040)
     f32("sg", 2 * NS); f32("wn", 64); f32("la", 8); f32("tw", 24)
@@ -37,7 +37,7 @@ def _scratch():
     mx("qz", 128); mx("qpr", 128); mx("qc", 1024); mx("qh", C + 2)
     for t in range(2):
         k = str(t)
-        f32("so" + k, 12); f32("stl" + k, 32); f32("rst" + k, 6)
+        f32("so" + k, 12); f32("stl" + k, 96); f32("rst" + k, 6)
         mx("land" + k, LAND); mx("yq" + k, NS); mx("rp" + k, 2 * OWN)
     for b in range(8):
         s["b%d" % b] = ("psum", [128, 512], "float32")
@@ -65,19 +65,13 @@ def _plan(T, topo):
         can = [c for c in topo.cores_of(cs[r]) if c != cs[r] and all(topo.may_write(c, cs[d]) for d in cross[r])]
         near = [c for c in can if topo.die(c) == topo.die(cs[r])]
         far = [c for c in can if topo.die(c) != topo.die(cs[r])]
-        relay.append([(far[0], 0, 0), (far[1], 2, 0), (near[0], 0, 1), (near[1], 2, 1)])
+        relay.append([(near[0], 0, 0), (near[1], 2, 0), (far[0], 0, 1), (far[1], 2, 1)])
     return cs, par, own, cross, kk, relay
 
 
 def _dst(topo, d, core):
     rid, pid = topo.addr(d, core)
     return DstId(rid=rid, pnc=pid)
-
-
-def _direct(topo, r, d, cs, own, kind):
-    i = (own[r].index(d) - own[r].index(r)) % 4 - 1
-    e = topo.engines(cs[r], cs[d])
-    return ((e[0:4], e[4:6], e[6:8]), (e[0:2], e[4:8], e[2:4]), (e[0:2], e[2:4], e[4:8]))[kind][i]
 
 
 def _u8(T, name, what, a, b):
@@ -87,9 +81,8 @@ def _u8(T, name, what, a, b):
 
 def _relay_program(g, core, T, topo, r, first, role, plan):
     cs, par, own, cross, kk, relay = plan
-    ids = [_dst(topo, cs[d], core) for d in cross[r][first:first + 2]]
+    ids = [[_dst(topo, cs[d], core) for d in [cross[r][o]] + ([own[r][o]] if role and own[r][o] != r else [])] for o in (first, first + 1)]
     eng = topo.engines(core, cs[cross[r][first]])
-    half = [eng[0:4], eng[4:8]]
     n, a = 0, L0 + NS * r
     for t in range(2):
         k = str(t)
@@ -99,10 +92,10 @@ def _relay_program(g, core, T, topo, r, first, role, plan):
             trs = []
             for i in range(2):
                 if kind == "t":
-                    src, dst = T["rst" + k][:, 3 * i:3 * i + 3], T["stl" + k][:, 4 * r:4 * r + 3]
+                    src, dst = T["rst" + k][:, 3 * i:3 * i + 3], T["stl" + k][:, 12 * r + 4:12 * r + 7]
                 else:
                     src, dst = _u8(T, "rp" + k, kind, OWN * i, OWN * i + OWN), _u8(T, "land" + k, kind, a, a + OWN)
-                trs.append(RemoteDMATransfer(dst_ids=[ids[i]], dma_engine_mask=_m(half[i]), remote_sem=sm, srcs=[src], dsts=[dst]))
+                trs.append(RemoteDMATransfer(dst_ids=ids[i], dma_engine_mask=_m(eng[4 * i:4 * i + 4]), remote_sem=sm, srcs=[src], dsts=[dst for d in ids[i]]))
             g.remote_dma_fused(trs, local_sem=T.sem.lr)
             n += len(eng)
     g.wait_ge(T.sem.lr, n)
@@ -174,11 +167,11 @@ def _rank_program(g, core, T, topo, r, plan):
     def quant(label, deps, out, a, b, tile, ta):
         do("v", label, deps, V.quantize_mx, T[out][:, a:b], T[out + "s"][:, a:b], T[tile][:, ta:ta + 4 * (b - a)])
 
-    def pickc(label, deps, out, a, b, win, wb, off, e, f):
-        cp(label + "c", deps, T[out][:, a:b].bitcast(dt.uint32), T[win][:, 0:wb].bitcast(dt.uint32).indirect(T[off][:, e:f]))
+    def pickc(label, deps, out, a, b, win, wa, wb, off, e, f):
+        cp(label + "c", deps, T[out][:, a:b].bitcast(dt.uint32), T[win][:, wa:wb].bitcast(dt.uint32).indirect(T[off][:, e:f]))
 
-    def picks(label, deps, out, a, b, win, wb, off, e, f):
-        do("s", label + "s", deps, S.activation, T[out + "s"][:, a:b], T[win + "s"][:, 0:wb].indirect(T[off][:, e:f]), ACT.Copy)
+    def picks(label, deps, out, a, b, win, wa, wb, off, e, f):
+        do("s", label + "s", deps, S.activation, T[out + "s"][:, a:b], T[win + "s"][:, wa:wb].indirect(T[off][:, e:f]), ACT.Copy)
 
     def pick(*a):
         pickc(*a)
@@ -218,60 +211,61 @@ def _rank_program(g, core, T, topo, r, plan):
     dma("s", "Lx0", [], T.x0[:, 0:512], T.x[:, 0:512])
     dma("q", "Lx1", [], T.x0[:, 512:1024], T.x[:, 512:1024])
     dma("s", "Lx2", [], T.x0[:, 1024:1536], T.x[:, 1024:1536])
-    dma("q", "Lw", ["Lu"], T.wqs[:], T.ws[:])
-    dma("q", "Lw", [], T.wq[:].bitcast(dt.uint8), T.wc[:])
-    dma("q", "Lv", ["Lw"], T.vt[:], T.v[:])
 
     iota("gp", T.tw[:, 16:17], [[0, 1]], 0, 1)
     iota("gp", T.tw[:, 0:16], [[-2, 2], [0, 8]], 2, 0)
     iota("gl", T.lu[:], [[16, 8]], 1, 0, True)
     iota("gm", T.mi[:], [[1, 128]], 0, 0)
-    iota("gz", T.wzi[:], [[0, 4], [1, 16], [0, 4]], 0, 0)
+    dma("q", "Lw", ["gm"], T.wqs[:], T.ws[:])
+    dma("q", "Lw", [], T.wq[:].bitcast(dt.uint8), T.wc[:])
+    dma("q", "Lv", ["Lw"], T.vt[:], T.v[:])
+    iota("gz", T.pr[:, C:C + 256], [[0, 4], [1, 16], [0, 4]], 0, 0)
     iota("gn", T.ni[:, 0:18], [[0, 3], [1, 6]], 0, 0)
     iota("gn", T.ni[:, 24:32], [[1, 8]], 0, 0)
     one = T.z[:, 224:736]
     iota("go", one, [[0, 512]], 1, 0)
-    iota("g0", T.z[:, 0:224], [[0, 224]], 0, 0)
-    iota("g0", T.ht[:, 0:8], [[0, 8]], 0, 0)
     iota("gd", T.sg[:, 0:NS], [[0, 12], [1, 16]], 0, 0)
-    do("g", "gs", ["go"], g.affine_select, T.seg[:], T.z[:, 224:224 + NS], [[0, 12], [1, 16]], ALU.not_equal, 0.0, 0, 0)
+    w("g", "go")
     pa = T.ct[:, 3587:4096:4]
     do("g", "ga", [], g.affine_select, T.ct[:, 3584:4096], one, [[16, 8], [1, 16], [200, 4]], ALU.is_equal, 0.0, 2 - 600, -1)
     do("g", "ga", ["ga"], g.affine_select, pa, pa, [[1, 8], [-1, 16]], ALU.not_equal, 0.0, 0, 0)
     do("g", "ga", ["ga"], g.affine_select, pa, pa, [[0, 16], [16, 8]], ALU.not_equal, 1.0, 0, -1)
     iota("gf", T.fi[:], [[1, 516]], -3, -4)
-    iota("gc", T.pr[:, C:512], [[0, 512 - C]], 0, 0)
     iota("gc", T.yt[:, 0:4], [[0, 4]], 0, 0)
     n8 = T.ni[:, 24:32]
 
-    fill("khc", T.hc[:], -STEP)
+    fill("khv", T.hv[:], -STEP)
+    for b in range(3):
+        act("khc", ["khv"], T.hc[:, b:1024:4], T.hv[:])
     fill("kl", T.lup[:, 0:8], 15)
+    fill("g0", T.z[:, 0:224], 0.0)
+    fill("g0", T.ht[:, 0:8], 0.0)
+    fill("g0", T.sr[:, 0:2], -1e29)
     do("v", "k0", ["gp"], V.tensor_tensor_scan, T.la[:, 0:8], T.tw[:, 0:8], T.tw[:, 8:16], T.tw[:, 16:17], ALU.mult, ALU.add)
-    cp("kl", ["gl"], T.lup[:, 8:16], T.lu[:])
     cp("k0", ["k0"], T.jc[:, 16:24], T.la[:, 0:8])
+    cp("kl", ["gl"], T.lup[:, 8:16], T.lu[:])
     w("v", "k0")
     for a, b, sel, mask in ((0, 8, slice(16, 24), 256), (8, 11, slice(18, 23, 2), 384), (11, 13, slice(18, 21, 2), 480), (13, 15, slice(16, 21, 4), 224)):
         ts("k0", [], T.jc[:, a:b], T.jc[:, sel], mask, ALU.bitwise_and)
     w("v", "k0")
     for a, b, d in ((0, 8, 256.0), (8, 11, 128.0), (11, 15, 32.0)):
         ts("k0", [], fc[:, a:b], T.jc[:, a:b], 1.0 / d, ALU.mult)
+    ts("k1", [], F("g7"), T.tw[:, 16:17], 112.0, ALU.is_equal, 128.0, ALU.mult)
     ts("k3", ["k0"], F("r1"), pv2, 4.0, ALU.mult, pv0, ALU.add)
     ts("k1", [], F("a0"), bit(4), -1.0, ALU.mult, 2.0, ALU.add)
     ts("k1", [], F("a1"), bit(5), -3.0, ALU.mult, 4.0, ALU.add)
     ts("k1", [], F("a2"), bit(6), -15.0, ALU.mult, 16.0, ALU.add)
     ts("k1", [], F("p0"), p15, 0.0, ALU.is_equal)
-    ts("k1", [], F("g7"), T.tw[:, 16:17], 112.0, ALU.is_equal, 128.0, ALU.mult)
+    quant("uq", ["Lu"], "uq", 0, 128, "ut", 0)
     ts("k1", ["k1"], F("ak"), F("a0"), F("a1"), ALU.mult, F("a2"), ALU.mult)
 
     def equal(label, deps, out, in_, tmp, col):
         act(label + "a", deps, tmp, in_, ACT.Abs, bias=col, scale=-1.0)
         return lambda: act(label, [label + "a"], out, tmp, ACT.Relu, bias=1.0, scale=-1.0)
 
-    second = [equal("ky", ["gz", "k0"], T.ct[:, 256:512], T.wzi[:], T.et[:, 256:512], p15),
-              equal("ky", [], T.ct[:, 0:128], T.wzi[:, 0:128], T.et[:, 0:128], r0),
-              equal("ky", ["k3"], T.ct[:, 128:256], T.wzi[:, 0:128], T.et[:, 128:256], F("r1"))]
-    for f in second:
-        f()
+    second = [equal("ky", ["gz", "k0"], T.ct[:, 256:512], T.pr[:, C:C + 256], T.et[:, 256:512], p15),
+              equal("ky", [], T.ct[:, 0:128], T.pr[:, C:C + 128], T.et[:, 0:128], r0),
+              equal("ky", ["k3"], T.ct[:, 128:256], T.pr[:, C:C + 128], T.et[:, 128:256], F("r1"))]
 
     todo = []
 
@@ -291,8 +285,7 @@ def _rank_program(g, core, T, topo, r, plan):
     for q in range(3):
         later("kz", ["k2"], T.zm[:, q:56:4], T.ni[:, 0:14], F("t%d" % q), ALU.is_equal)
     later("kz", [], T.zm[:, 3:24:4], T.ni[:, 0:6], F("t3"), ALU.is_equal)
-    todo.append(lambda: fill("kh", T.sr[:, 0:2], -1e29))
-    later("kc", [], T.wn[:, 32:51:9], T.ni[:, 0:3], 16.0, ALU.mult, p15, ALU.add)
+    later("kc", [], T.wn[:, 60:63], T.ni[:, 0:3], 16.0, ALU.mult, p15, ALU.add)
     later("kg", [], F("g4"), grp, 4.0, ALU.mult)
     later("kn", [], F("c0"), bit(0), 1.0, ALU.add)
     later("kn", [], F("c1"), bit(1), 3.0, ALU.mult, 1.0, ALU.add)
@@ -316,25 +309,29 @@ def _rank_program(g, core, T, topo, r, plan):
     later("kn", ["kn"], F("w2"), F("w1"), F("ne"), ALU.mult, 256.0, ALU.subtract)
     later("kn", ["kn"], F("w3"), F("w2"), F("lo"), ALU.mult)
 
-    gap(2)
-    quant("uq", ["Lu"], "uq", 0, 128, "ut", 0)
+    pick("up", ["uq", "kl"], "up", 0, 128, "uq", 0, 128, "lup", 0, 8)
     ts("k1", ["k1", "gm"], T.mj[:], T.mi[:], F("ak"), ALU.mult, F("p0"), ALU.mult)
-    pick("up", ["uq", "kl"], "up", 0, 128, "uq", 128, "lup", 0, 8)
+    quant("qx0", ["Lx0"], "qx0", 0, 128, "x0", 0)
     ts("k1", ["k1"], T.mj[:], T.mj[:], 128, ALU.bitwise_and)
-    for c in range(3):
-        quant("qx%d" % c, ["Lx%d" % c], "qx0", 128 * c, 128 * c + 128, "x0", 512 * c)
-    pick("uo", ["uq"], "up", 128, 256, "uq", 128, "lup", 8, 16)
-    ts("k1", ["k1", "khc"], T.hc[:, 3:512:4], T.mj[:], -16 * STEP, ALU.mult)
+    pick("uo", ["uq"], "up", 128, 256, "uq", 0, 128, "lup", 8, 16)
+    for f in second:
+        f()
+    quant("qx1", ["Lx1"], "qx0", 128, 256, "x0", 512)
+    ts("k1", ["k1"], T.hc[:, 3:512:4], T.mj[:], -16 * STEP, ALU.mult)
+    quant("qx2", ["Lx2"], "qx0", 256, 384, "x0", 1024)
     ts("k1", [], T.hc[:, 515:1024:4], T.mj[:], F("g7"), ALU.add, -16 * STEP, ALU.mult)
+    gap()
+    quant("qhc", ["k1", "khc"], "qhc", 0, 256, "hc", 0)
 
-    def unpackers():
-        act("kea", ["gf"], T.et[:, 0:516], T.fi[:], ACT.Abs)
-        for b in range(4):
+    def unpackers(*bs):
+        if 0 in bs:
+            act("kea", ["gf", "ky"], T.et[:, 0:516], T.fi[:], ACT.Abs)
+        for b in bs:
             act("kes", ["kea"], T.ct[:, 1536 + 512 * b:2048 + 512 * b], T.et[:, 3 - b:515 - b], ACT.Relu, bias=1.0, scale=-1.0)
 
     def weighted(label, deps, a, col):
         equal(label, deps, T.ct[:, a:a + 512], T.gw[:], T.et[:, 520:1032], F("g4"))()
-        act(label, [label, "kn"], T.ct[:, a:a + 512], T.ct[:, a:a + 512], ACT.Identity, scale=col)
+        return lambda: act(label, [label, "kn"], T.ct[:, a:a + 512], T.ct[:, a:a + 512], ACT.Identity, scale=col)
 
     e_off = topo.engines(core, cs[peers[0]])
     e_on = [e for e in topo.engines(core, relay[r][0][0]) if e not in e_off]
@@ -365,8 +362,8 @@ def _rank_program(g, core, T, topo, r, plan):
         if t == 0:
             tr(0, 0)
             tr(1, 1)
+            mm("ms0", ["upc", "ups", "qx2"], 3, "up", 0, qx, 0, C)
             tr(2, 2)
-            mm("ms0", ["upc", "ups"], 3, "up", 0, qx, 0, C)
             mm("mth", ["uoc", "uos"], 4, "up", 128, qx, 0, C)
             mm("ms1", [], 5, "up", 0, qx, 0, C)
             mm("mp", [], 6, "uq", 0, qx, 0, C)
@@ -376,8 +373,9 @@ def _rank_program(g, core, T, topo, r, plan):
             act("thr", ["mth"], T.thr[:], bank[4][:, 0:C])
             sign(0, 0, C, bank[5][:, 0:C], ["ms1"])
             act("sr", [], sr[:, 2:C + 2], bank[5][:, 0:C])
+            gap()
             tt("pf", ["mp", "thr"], fl[:, 3:4 * C:4], bank[6][:, 0:C], T.thr[:], ALU.is_le)
-            quant("qhc", ["k1"], "qhc", 0, 256, "hc", 0)
+            gap(2)
             layer(0, 7, ["stc"])
             layer(1, 0, [])
             kbk = (4, 5)
@@ -391,7 +389,8 @@ def _rank_program(g, core, T, topo, r, plan):
                 if c < 2:
                     act("stc", ["mt%d" % c], T.stc[:, c:c + 1], bank[0][:, 15:16])
                 else:
-                    mm("mp", [], 7, "uq", 0, qx, 0, C)
+                    mm("mp1", ["h0"], 3, "uq", 0, qx, lo, hi)
+                    tt("pf", ["mp", "thr"], fl[:, 3:4 * lo:4], bank[7][:, 0:lo], T.thr[:, 0:lo], ALU.is_le)
                     less(2, 0, lo, sr[:, 2:2 + lo], 0, ["sr", "mt2"])
                 act("sr", ["ms0"], sr[:, 2 + lo:2 + hi], bank[1][:, 0:128])
                 act("thr", ["mth"], T.thr[:, lo:hi], bank[2][:, 0:128])
@@ -399,12 +398,14 @@ def _rank_program(g, core, T, topo, r, plan):
                     sign(j, lo, hi, bank[1][:, 0:128], [])
                 if c == 1:
                     sign(1, 0, lo, sr[:, 2:2 + lo], ["sr"])
-                if c != 1:
-                    w("p", "h0")
+                    mm("mp", [], 7, "uq", 0, qx, 0, hi)
+                if c == 0:
                     for b in range(4):
-                        layer(b, 3 + b, [], 64 * c, hi)
-            tt("pf", ["mp", "thr"], fl[:, 3:4 * C:4], bank[7][:, 0:C], T.thr[:], ALU.is_le)
+                        layer(b, 3 + b, [], lo, hi)
             less(2, 256, C, sr[:, 258:C + 2], 0, ["sr"])
+            tt("pf", ["mp1", "thr"], fl[:, 3 + 1024:4 * C:4], bank[3][:, 0:128], T.thr[:, 256:C], ALU.is_le)
+            for b in range(4):
+                layer(b, (4, 5, 6, 3)[b], ["pf"] if b == 3 else [], 128, C)
             kbk = (1, 2)
         quant("qfl", ["pf", "sg", "ls1", "ls2"], "qfl", 0, C, "fl", 0)
         if t:
@@ -415,7 +416,8 @@ def _rank_program(g, core, T, topo, r, plan):
             layer(2, 1, [])
             layer(3, 2, [])
             equal("kd", ["gd"], T.dm[:], T.sg[:, 0:NS], T.et[:, 520:520 + NS], p15)()
-            gap(7)
+            act("gs", [], T.seg[:], T.sg[:, 0:NS], ACT.Sign)
+            gap(5)
         for h, (a, b) in enumerate(((0, 24), (24, 56))):
             do("v", "sc%d" % h, ["mk%d" % h, "go"], V.tensor_tensor_scan, T.sc[:, C * h:C * h + C], T.z[:, 224:224 + C], bank[kbk[h]][:, 0:C], -STEP * 1024, ALU.add, ALU.max)
         for h, (a, b) in enumerate(((0, 24), (24, 56))):
@@ -436,25 +438,32 @@ def _rank_program(g, core, T, topo, r, plan):
         for q in range(4):
             src = bank[3][32 * q:32 * q + 32, q:48:4] if q < 3 else bank[3][96:128, 11:56:4]
             ts("ls", [], T.ls[32 * q:32 * q + 32, :], src, -1.0, ALU.mult, float(C + 1), ALU.add)
-        picks("c", ["ls", "qh"], land, c0, c0 + NS, "qh", C + 2, "ls", 0, 12)
         so, stl = T["so" + k], T["stl" + k]
+        picks("c", ["ls", "qh"], land, c0, c0 + NS, "qh", 0, C + 2, "ls", 0, 12)
         gap()
-        tt("sa", ["ls", "sr", "kd", "kh"], T.sg[:, 0:NS], sr[:, 0:C + 2].indirect(T.ls[:, 0:12]), T.dm[:], ALU.mult)
+        tt("sa", ["ls", "sr", "kd", "g0", "gs"], T.sg[:, 0:NS], sr[:, 0:C + 2].indirect(T.ls[:, 0:12]), T.dm[:], ALU.mult)
         gap()
-        do("v", "sb", ["sa", "gs"], V.tensor_tensor_scan, T.sg[:, NS:2 * NS], T.seg[:], T.sg[:, 0:NS], 0.0, ALU.mult, ALU.add)
+        do("v", "sb", ["sa"], V.tensor_tensor_scan, T.sg[:, NS:2 * NS], T.seg[:], T.sg[:, 0:NS], 0.0, ALU.mult, ALU.add)
         gap()
         cp("so", ["sb"], so[:], T.sg[:, NS + 15:2 * NS:16])
-        pickc("c", ["qh"], land, c0, c0 + NS, "qh", C + 2, "ls", 0, 12)
-        cp("sown", ["so"], stl[:, 4 * r:4 * r + 3], so[:, 3 * mk:3 * mk + 3])
-        for kind, (what, sm, lb) in enumerate((("s", "ps", "cs"), ("t", "st", "so"), ("", "pc", "cc"))):
-            def piece(o, n):
-                return so[:, 3 * o:3 * (o + n)] if what == "t" else u8(land, what, c0 + OWN * o, c0 + OWN * (o + n))
-            rl = (2, 3) if what == "s" else (0, 1)
-            send([lb], sm + k, [([rid[j]], e_on[4 * i:4 * i + 4], piece(relay[r][j][1], 2), T["rst" + k][:] if what == "t" else u8("rp" + k, what, 0, 2 * OWN))
-                                for i, j in enumerate(rl)])
-            send([], sm + k, [([pid[i]], _direct(topo, r, d, cs, own, kind), piece(kk[d], 1), stl[:, 4 * r:4 * r + 3] if what == "t" else u8(land, what, mine, mine + OWN))
-                              for i, d in enumerate(peers)])
-            cnt[sm + k] = sum(len(_direct(topo, s, r, cs, own, kind)) for s in peers) + 16
+        pickc("c", ["qh"], land, c0, c0 + NS, "qh", 0, C + 2, "ls", 0, 12)
+        cp("sown", [], stl[:, 12 * r + 4:12 * r + 7], T.sg[:, NS + 15 + OWN * mk:NS + OWN * mk + OWN:16])
+
+        def piece(what, o, n):
+            return so[:, 3 * o:3 * (o + n)] if what == "t" else u8(land, what, c0 + OWN * o, c0 + OWN * (o + n))
+
+        def relayed(what, which):
+            return [([rid[j]], e_on[4 * i:4 * i + 4], piece(what, relay[r][j][1], 2), T["rst" + k][:] if what == "t" else u8("rp" + k, what, 0, 2 * OWN))
+                    for i, j in enumerate(which)]
+
+        e = e_off
+        send(["cs"], "ps" + k, [([rid[2 + i]], e[4 * i:4 * i + 4], piece("s", 2 * i, 2), u8("rp" + k, "s", 0, 2 * OWN)) for i in range(2)])
+        send(["so"], "st" + k, relayed("t", (0, 1)) + [([pid[i]], (e[0:4], e[4:6], e[6:8])[i], piece("t", kk[d] // 2 * 2, 2), stl[:, 12 * r + 4 - 3 * (kk[d] % 2):12 * r + 10 - 3 * (kk[d] % 2)])
+                                                      for i, d in enumerate(peers)])
+        send(["cc"], "pc" + k, relayed("", (0, 1)))
+        for which in ((0, 1), (2,)):
+            send([], "pc" + k, [([pid[i]], (e[0:4], e[4:8], e)[i], piece("", kk[peers[i]], 1), u8(land, "", mine, mine + OWN)) for i in which])
+        cnt["ps" + k], cnt["st" + k], cnt["pc" + k] = 4 * 7, 8 + 16, 16 + 16
 
         def offsets():
             mm("ml", ["qpr", "qwl"], 0, "qc", 128, "qpr", 0, 128)
@@ -463,17 +472,17 @@ def _rank_program(g, core, T, topo, r, plan):
         if t == 0:
             iota("gw", T.gw[:], [[1, 32], [0, 4], [-1, 4]], 0, 0)
             quant("qpa", ["ga"], "qc", 896, 1024, "ct", 3584)
-            unpackers()
+            unpackers(0, 1, 2, 3)
         mm("ma", ["qpa", "ht"], 6, "qc", 896, "qfl", 0, C)
         gap(6)
         ts("pr", ["ma"], T.pr[:, 0:C], bank[6][:, 0:C], 0.0, ALU.is_equal)
         gap(99)
         if t == 0:
-            weighted("kw", ["gw", "kg"], 512, F("w3"))
+            weigh = weighted("kw", ["gw", "kg"], 512, F("w3"))
             quant("qe", ["kes"], "qc", 384, 896, "ct", 1536)
             quant("qpr", ["pr", "gc"], "qpr", 0, 128, "pr", 0)
         else:
-            weighted("kv", ["gv"], 1024, F("wl"))
+            weighted("kv", ["gv"], 1024, F("wl"))()
             quant("qpr", ["pr"], "qpr", 0, 128, "pr", 0)
             cp("pw", [], fl[:, 3:4 * C:4], T.pr[:, 0:C])
             offsets()
@@ -481,21 +490,19 @@ def _rank_program(g, core, T, topo, r, plan):
         wn = T.wn
         w("v", "st" + k, "sown", "kc")
         for c in range(3):
-            do("v", "w1", [], V.tensor_tensor_scan, wn[:, 8 * c:8 * c + 8], stl[:, c:32:4], stl[:, c:32:4], -1e29, ALU.max, ALU.max)
-        w("v", "w1")
+            do("v", "w1", [], V.tensor_tensor_scan, wn[:, 8 * c:8 * c + 8], stl[:, 4 + c:96:12], stl[:, 4 + c:96:12], -1e29, ALU.max, ALU.max)
+            act("w2%d" % c, ["w1"], wn[:, 24 + 8 * c:32 + 8 * c], wn[:, 8 * c:8 * c + 8], ACT.Sign, bias=wn[:, 8 * c + 7:8 * c + 8], scale=-1.0,
+                accum_out=wn[:, 56 + c:57 + c])
         for c in range(3):
-            ts("w1", [], wn[:, 24 + 9 * c:32 + 9 * c], wn[:, 8 * c:8 * c + 8], wn[:, 8 * c + 7:8 * c + 8], ALU.is_lt, float(NS), ALU.mult)
-        w("v", "w1")
-        for c in range(3):
-            do("v", "w1", [], V.tensor_reduce, wn[:, 56 + c:57 + c], wn[:, 24 + 9 * c:33 + 9 * c], AxisListType.X, ALU.add)
-        ts("tl", ["w1"], T.tl[:, 0:3], wn[:, 56:59], float(L0), ALU.add)
+            ts("tl", ["w2%d" % c], T.tl[:, c:c + 1], wn[:, 56 + c:57 + c], float(NS), ALU.mult, wn[:, 60 + c:61 + c], ALU.add)
         a = OWN * mk
-        pickc("t", ["tl", "cc", "pc" + k], yq, a, a + OWN, land, LAND, "tl", 0, 3)
-        picks("t", ["tl", "cs", "ps" + k], yq, a, a + OWN, land, LAND, "tl", 0, 3)
-        for what, sm, lb in (("", "yc", "tc"), ("s", "ys", "ts")):
+        pickc("t", ["tl", "cc", "pc" + k], yq, a, a + OWN, land, L0, LAND, "tl", 0, 3)
+        picks("t", ["tl", "cs", "ps" + k], yq, a, a + OWN, land, L0, LAND, "tl", 0, 3)
+        for what, sm, lb in (("", "yc", "tc"), ("s", "ys", "ts"))[::1 - 2 * t]:
             send([lb], sm + k, [(pid, e_off, u8(yq, what, a, a + OWN), u8(yq, what, a, a + OWN))])
             cnt[sm + k] = 3 * len(e_off)
         if t == 0:
+            weigh()
             quant("qwl", ["kw"], "qc", 128, 256, "ct", 512)
             offsets()
             quant("vq", ["Lv"], "vq", 0, 128, "vt", 0)

from concourse.bass import DstId, RemoteDMATransfer
from concourse.mybir import dt, AluOpType, ActivationFunctionType, AxisListType

ALU, ACT = AluOpType, ActivationFunctionType
NR = 8
C = 384
NS = 192
OWN = 48
L0 = 160
LAND = L0 + NR * NS
STEP = 512.0


def _scratch():
    s = {}

    def bf(name, n): s[name] = ("sbuf", [128, n], "bfloat16")
    def f32(name, n): s[name] = ("sbuf", [128, n], "float32")
    def i32(name, n): s[name] = ("sbuf", [128, n], "int32")
    def u16(name, n): s[name] = ("sbuf", [128, n], "uint16")

    def mx(name, n):
        s[name] = ("sbuf", [128, n], "float8_e4m3fn_x4")
        s[name + "s"] = ("sbuf", [128, n], "uint8")

    bf("ut", 512); bf("vt", 512)
    for t in range(3):
        bf("x%d" % t, 4 * C); mx("qx%d" % t, C)
    bf("fl", 4 * C); bf("hc", 1024); bf("z", 224 + 512); bf("ht", 4 * (C + 2)); bf("pr", C + 256); bf("ct", 4096); bf("yt", 4 * NS + 16)
    bf("hv", 256); bf("seg", NS); bf("dm", NS)
    f32("thr", C); f32("sr", C + 2); f32("sc", 2 * C); f32("fc", 96); f32("ni", 32); f32("zm", 56); f32("stc", 2)
    f32("yo", C); f32("wlb", C); f32("mi", 128); f32("fi", 516); f32("gw", 512); f32("et", 1040)
    f32("sg", 2 * NS); f32("wn", 64); f32("la", 8); f32("tw", 24)
    i32("jc", 24); i32("mj", 128); i32("lu", 8); i32("ai", 56); i32("dg", 224)
    u16("lup", 16); u16("ls", 12); u16("off", 96); u16("tl", 4)
    mx("uq", 128); mx("up", 256); mx("vq", 128); mx("wq", 512); mx("qfl", C); mx("qhc", 256)
    mx("qz", 128); mx("qpr", 128); mx("qc", 1024); mx("qh", C + 2)
    for t in range(2):
        k = str(t)
        f32("so" + k, 12); f32("stl" + k, 96); f32("rst" + k, 6)
        mx("land" + k, LAND); mx("yq" + k, NS); mx("rp" + k, 2 * OWN)
    for b in range(8):
        s["b%d" % b] = ("psum", [128, 512], "float32")
    return s


SCRATCH = _scratch()
_REMOTE = ["st", "pc", "ps", "yc", "ys"]
_RSEMS = [n + str(t) for t in range(2) for n in _REMOTE] + ["lr"]
SEMAPHORES = _RSEMS + ["c%d" % i for i in range(139)]


def _m(engines):
    return sum(1 << e for e in engines)


def _plan(T, topo):
    cs = list(T.cores)
    par = [0 if r == 0 or topo.may_write(cs[0], cs[r]) else 1 for r in range(NR)]
    own = [[s for s in range(NR) if par[s] == par[r]] for r in range(NR)]
    cross = [[s for s in range(NR) if par[s] != par[r]] for r in range(NR)]
    kk = [own[r].index(r) for r in range(NR)]
    relay = []
    for r in range(NR):
        can = [c for c in topo.cores_of(cs[r]) if c != cs[r] and all(topo.may_write(c, cs[d]) for d in cross[r])]
        near = [c for c in can if topo.die(c) == topo.die(cs[r])]
        far = [c for c in can if topo.die(c) != topo.die(cs[r])]
        relay.append([(near[0], 0, 0), (near[1], 2, 0), (far[0], 0, 1), (far[1], 2, 1)])
    return cs, par, own, cross, kk, relay


def _dst(topo, d, core):
    rid, pid = topo.addr(d, core)
    return DstId(rid=rid, pnc=pid)


def _u8(T, name, what, a, b):
    v = T[name + what][:, a:b]
    return v if what else v.bitcast(dt.uint8)


def _relay_program(g, core, T, topo, r, first, role, plan):
    cs, par, own, cross, kk, relay = plan
    ids = [[_dst(topo, cs[d], core) for d in [cross[r][o]] + ([own[r][o]] if role and own[r][o] != r else [])] for o in (first, first + 1)]
    eng = topo.engines(core, cs[cross[r][first]])
    n, a = 0, L0 + NS * r
    for t in range(2):
        k = str(t)
        for kind in (("s",) if role else ("t", "")):
            sm = T.sem[{"": "pc", "s": "ps", "t": "st"}[kind] + k]
            g.wait_ge(sm, 4)
            trs = []
            for i in range(2):
                if kind == "t":
                    src, dst = T["rst" + k][:, 3 * i:3 * i + 3], T["stl" + k][:, 12 * r + 4:12 * r + 7]
                else:
                    src, dst = _u8(T, "rp" + k, kind, OWN * i, OWN * i + OWN), _u8(T, "land" + k, kind, a, a + OWN)
                trs.append(RemoteDMATransfer(dst_ids=ids[i], dma_engine_mask=_m(eng[4 * i:4 * i + 4]), remote_sem=sm, srcs=[src], dsts=[dst for d in ids[i]]))
            g.remote_dma_fused(trs, local_sem=T.sem.lr)
            n += len(eng)
    g.wait_ge(T.sem.lr, n)


def rank_program(g, core, T, topo):
    plan = _plan(T, topo)
    rank = T.rank_of(core)
    if rank is None:
        for r in range(NR):
            for c, first, role in plan[5][r]:
                if c == core:
                    _relay_program(g, core, T, topo, r, first, role, plan)
        return
    _rank_program(g, core, T, topo, rank, plan)


def _rank_program(g, core, T, topo, r, plan):
    cs, par, own, cross, kk, relay = plan
    mk = kk[r]
    peers = [own[r][(mk + i) % 4] for i in (1, 2, 3)]
    V, S, P = g.vector, g.scalar, g.tensor
    names, cnt, seen, done, cols = {}, {}, {}, {}, {}
    bank = [T["b%d" % i] for i in range(8)]
    qid = {"g": g, "v": V, "s": S, "p": P, "q": g.sync}

    def sem(label):
        if label in _RSEMS:
            return T.sem[label]
        if label not in names:
            names[label] = "c%d" % len(names)
        return T.sem[names[label]]

    def w(q, *labels):
        for lb in labels:
            n = cnt.get(lb, 0)
            if n and seen.get((q, lb), 0) < n:
                qid[q].wait_ge(sem(lb), n)
                seen[(q, lb)] = n
                done[lb] = max(done.get(lb, 0), n)

    def do(q, label, deps, method, *args, **kw):
        w(q, *deps)
        n = kw.pop("n", 1)
        method(*args, **kw).then_inc(sem(label), n)
        cnt[label] = cnt.get(label, 0) + n

    def dma(q, label, deps, out, in_):
        do(q, label, deps, qid[q].dma_start, out, in_, n=16)

    def ts(label, deps, out, in0, s1, op0, s2=None, op1=None):
        if op1 is None:
            do("v", label, deps, V.tensor_scalar, out, in0, s1, None, op0)
        else:
            do("v", label, deps, V.tensor_scalar, out, in0, s1, s2, op0, op1)

    def tt(label, deps, out, in0, in1, op):
        do("v", label, deps, V.tensor_tensor, out, in0, in1, op)

    def cp(label, deps, out, in_):
        do("v", label, deps, V.tensor_copy, out, in_)

    def fill(label, out, c):
        do("v", label, [], V.memset, out, c)

    def mm(label, deps, b, lhs, la, rhs, ra, rb):
        do("p", label, deps, P.matmul_mx, bank[b][:, 0:rb - ra], T[lhs][:, la:la + 128], T[lhs + "s"][:, la:la + 128], T[rhs][:, ra:rb], T[rhs + "s"][:, ra:rb], True, True)

    def quant(label, deps, out, a, b, tile, ta):
        do("v", label, deps, V.quantize_mx, T[out][:, a:b], T[out + "s"][:, a:b], T[tile][:, ta:ta + 4 * (b - a)])

    def pickc(label, deps, out, a, b, win, wa, wb, off, e, f):
        cp(label + "c", deps, T[out][:, a:b].bitcast(dt.uint32), T[win][:, wa:wb].bitcast(dt.uint32).indirect(T[off][:, e:f]))

    def picks(label, deps, out, a, b, win, wa, wb, off, e, f):
        do("s", label + "s", deps, S.activation, T[out + "s"][:, a:b], T[win + "s"][:, wa:wb].indirect(T[off][:, e:f]), ACT.Copy)

    def pick(*a):
        pickc(*a)
        picks(*a)

    def act(label, deps, out, in_, func=ACT.Copy, **kw):
        do("s", label, deps, S.activation, out, in_, func, **kw)

    def send(deps, sm, trs):
        w("g", *deps)
        g.remote_dma_fused([RemoteDMATransfer(dst_ids=ids, dma_engine_mask=_m(e), remote_sem=T.sem[sm], srcs=[src], dsts=[dst for i in ids])
                            for ids, e, src, dst in trs], local_sem=T.sem.lr)
        cnt["lr"] = cnt.get("lr", 0) + sum(len(e) for ids, e, src, dst in trs)

    def u8(name, what, a, b):
        return _u8(T, name, what, a, b)

    def iota(label, out, pattern, base, ch, whole=False):
        if whole:
            do("g", label, [], g.iota, out, pattern, base, ch)
        else:
            do("g", label, [], g.iota, out, pattern, base, ch, allow_small_or_imprecise_dtypes=True)

    fc = T.fc

    def F(name, n=1):
        if name not in cols:
            cols[name] = 16 + len(cols)
        return fc[:, cols[name]:cols[name] + n]

    def bit(j):
        return fc[:, 7 - j:8 - j]

    pv2, pv1, pv0, r0, p15, grp, kb = [fc[:, 8 + i:9 + i] for i in range(7)]

    dma("q", "Lu", [], T.ut[:], T.u[:])
    dma("s", "Lx0", [], T.x0[:, 0:512], T.x[:, 0:512])
    dma("q", "Lx1", [], T.x0[:, 512:1024], T.x[:, 512:1024])
    dma("s", "Lx2", [], T.x0[:, 1024:1536], T.x[:, 1024:1536])

    iota("gp", T.tw[:, 16:17], [[0, 1]], 0, 1)
    iota("gp", T.tw[:, 0:16], [[-2, 2], [0, 8]], 2, 0)
    iota("gl", T.lu[:], [[16, 8]], 1, 0, True)
    iota("gm", T.mi[:], [[1, 128]], 0, 0)
    dma("q", "Lw", ["gm"], T.wqs[:], T.ws[:])
    dma("q", "Lw", [], T.wq[:].bitcast(dt.uint8), T.wc[:])
    dma("q", "Lv", ["Lw"], T.vt[:], T.v[:])
    iota("gz", T.pr[:, C:C + 256], [[0, 4], [1, 16], [0, 4]], 0, 0)
    iota("gn", T.ni[:, 0:18], [[0, 3], [1, 6]], 0, 0)
    iota("gn", T.ni[:, 24:32], [[1, 8]], 0, 0)
    one = T.z[:, 224:736]
    iota("go", one, [[0, 512]], 1, 0)
    iota("gd", T.sg[:, 0:NS], [[0, 12], [1, 16]], 0, 0)
    w("g", "go")
    pa = T.ct[:, 3587:4096:4]
    do("g", "ga", [], g.affine_select, T.ct[:, 3584:4096], one, [[16, 8], [1, 16], [200, 4]], ALU.is_equal, 0.0, 2 - 600, -1)
    do("g", "ga", ["ga"], g.affine_select, pa, pa, [[1, 8], [-1, 16]], ALU.not_equal, 0.0, 0, 0)
    do("g", "ga", ["ga"], g.affine_select, pa, pa, [[0, 16], [16, 8]], ALU.not_equal, 1.0, 0, -1)
    iota("gf", T.fi[:], [[1, 516]], -3, -4)
    iota("gc", T.yt[:, 0:4], [[0, 4]], 0, 0)
    n8 = T.ni[:, 24:32]

    fill("khv", T.hv[:], -STEP)
    for b in range(3):
        act("khc", ["khv"], T.hc[:, b:1024:4], T.hv[:])
    fill("kl", T.lup[:, 0:8], 15)
    fill("g0", T.z[:, 0:224], 0.0)
    fill("g0", T.ht[:, 0:8], 0.0)
    fill("g0", T.sr[:, 0:2], -1e29)
    do("v", "k0", ["gp"], V.tensor_tensor_scan, T.la[:, 0:8], T.tw[:, 0:8], T.tw[:, 8:16], T.tw[:, 16:17], ALU.mult, ALU.add)
    cp("k0", ["k0"], T.jc[:, 16:24], T.la[:, 0:8])
    cp("kl", ["gl"], T.lup[:, 8:16], T.lu[:])
    w("v", "k0")
    for a, b, sel, mask in ((0, 8, slice(16, 24), 256), (8, 11, slice(18, 23, 2), 384), (11, 13, slice(18, 21, 2), 480), (13, 15, slice(16, 21, 4), 224)):
        ts("k0", [], T.jc[:, a:b], T.jc[:, sel], mask, ALU.bitwise_and)
    w("v", "k0")
    for a, b, d in ((0, 8, 256.0), (8, 11, 128.0), (11, 15, 32.0)):
        ts("k0", [], fc[:, a:b], T.jc[:, a:b], 1.0 / d, ALU.mult)
    ts("k1", [], F("g7"), T.tw[:, 16:17], 112.0, ALU.is_equal, 128.0, ALU.mult)
    ts("k3", ["k0"], F("r1"), pv2, 4.0, ALU.mult, pv0, ALU.add)
    ts("k1", [], F("a0"), bit(4), -1.0, ALU.mult, 2.0, ALU.add)
    ts("k1", [], F("a1"), bit(5), -3.0, ALU.mult, 4.0, ALU.add)
    ts("k1", [], F("a2"), bit(6), -15.0, ALU.mult, 16.0, ALU.add)
    ts("k1", [], F("p0"), p15, 0.0, ALU.is_equal)
    quant("uq", ["Lu"], "uq", 0, 128, "ut", 0)
    ts("k1", ["k1"], F("ak"), F("a0"), F("a1"), ALU.mult, F("a2"), ALU.mult)

    def equal(label, deps, out, in_, tmp, col):
        act(label + "a", deps, tmp, in_, ACT.Abs, bias=col, scale=-1.0)
        return lambda: act(label, [label + "a"], out, tmp, ACT.Relu, bias=1.0, scale=-1.0)

    second = [equal("ky", ["gz", "k0"], T.ct[:, 256:512], T.pr[:, C:C + 256], T.et[:, 256:512], p15),
              equal("ky", [], T.ct[:, 0:128], T.pr[:, C:C + 128], T.et[:, 0:128], r0),
              equal("ky", ["k3"], T.ct[:, 128:256], T.pr[:, C:C + 128], T.et[:, 128:256], F("r1"))]

    todo = []

    def later(label, deps, *a):
        todo.append(lambda: ts(label, deps, *a))

    def gap(n=1):
        for i in range(min(n, len(todo))):
            todo.pop(0)()

    F("t2"), F("t1"), F("t0")
    later("k2", [], F("b6"), bit(6), -2.0, ALU.add)
    later("k2", [], F("n6"), bit(6), -100.0, ALU.mult, 102.0, ALU.add)
    later("k2", ["k2"], F("t2", 3), fc[:, 8:11], 2.0, ALU.mult, F("b6"), ALU.add)
    later("k2", [], F("t3"), pv2, F("n6"), ALU.add)
    later("kz", ["gn"], T.zm[:, 27:56:4], n8, grp, ALU.is_equal)
    for q in range(3):
        later("kz", ["k2"], T.zm[:, q:56:4], T.ni[:, 0:14], F("t%d" % q), ALU.is_equal)
    later("kz", [], T.zm[:, 3:24:4], T.ni[:, 0:6], F("t3"), ALU.is_equal)
    later("kc", [], T.wn[:, 60:63], T.ni[:, 0:3], 16.0, ALU.mult, p15, ALU.add)
    later("kg", [], F("g4"), grp, 4.0, ALU.mult)
    later("kn", [], F("c0"), bit(0), 1.0, ALU.add)
    later("kn", [], F("c1"), bit(1), 3.0, ALU.mult, 1.0, ALU.add)
    later("kn", [], F("c2"), bit(2), 15.0, ALU.mult, 1.0, ALU.add)
    later("kn", [], F("d"), kb, grp, ALU.subtract, bit(4), ALU.add)
    later("kn", [], F("u"), grp, 6.0, ALU.is_ge, 1.0, ALU.add)
    later("kn", [], F("ne"), kb, grp, ALU.not_equal)
    later("kn", [], F("lo"), p15, 8.0, ALU.is_lt, 4.0, ALU.mult)
    later("kn", [], F("k7"), kb, 7.0, ALU.is_equal, -64.0, ALU.mult)
    later("kn", ["kn"], F("pw"), F("c0"), F("c1"), ALU.mult, F("c2"), ALU.mult)
    later("kn", [], F("gt"), F("d"), 1.0, ALU.is_gt, 0.25, ALU.mult)
    later("kn", [], F("u0"), F("u"), F("c0"), ALU.mult, 32.0, ALU.mult)
    later("kn", [], F("a5"), F("u"), -2.0, ALU.add, F("k7"), ALU.mult)
    later("kn", [], F("ub"), F("u"), bit(4), ALU.mult, 128.0, ALU.mult)
    later("kn", ["kn"], F("fa"), F("d"), 0.0, ALU.is_lt, F("gt"), ALU.add)
    later("kn", [], F("ob"), F("ub"), 4.0, ALU.add, pv0, ALU.add)
    later("kn", ["kn"], F("a3"), F("fa"), F("pw"), ALU.mult, F("a5"), ALU.add)
    later("kn", [], F("a4"), F("fa"), 0.0, ALU.is_equal, F("u0"), ALU.mult)
    later("kn", [], F("wl"), F("ne"), F("pw"), ALU.mult, F("lo"), ALU.mult)
    later("kn", ["kn"], F("w1"), F("a3"), F("a4"), ALU.add, 256.0, ALU.add)
    later("kn", ["kn"], F("w2"), F("w1"), F("ne"), ALU.mult, 256.0, ALU.subtract)
    later("kn", ["kn"], F("w3"), F("w2"), F("lo"), ALU.mult)

    pick("up", ["uq", "kl"], "up", 0, 128, "uq", 0, 128, "lup", 0, 8)
    ts("k1", ["k1", "gm"], T.mj[:], T.mi[:], F("ak"), ALU.mult, F("p0"), ALU.mult)
    quant("qx0", ["Lx0"], "qx0", 0, 128, "x0", 0)
    ts("k1", ["k1"], T.mj[:], T.mj[:], 128, ALU.bitwise_and)
    pick("uo", ["uq"], "up", 128, 256, "uq", 0, 128, "lup", 8, 16)
    for f in second:
        f()
    quant("qx1", ["Lx1"], "qx0", 128, 256, "x0", 512)
    ts("k1", ["k1"], T.hc[:, 3:512:4], T.mj[:], -16 * STEP, ALU.mult)
    quant("qx2", ["Lx2"], "qx0", 256, 384, "x0", 1024)
    ts("k1", [], T.hc[:, 515:1024:4], T.mj[:], F("g7"), ALU.add, -16 * STEP, ALU.mult)
    gap()
    quant("qhc", ["k1", "khc"], "qhc", 0, 256, "hc", 0)

    def unpackers(*bs):
        if 0 in bs:
            act("kea", ["gf", "ky"], T.et[:, 0:516], T.fi[:], ACT.Abs)
        for b in bs:
            act("kes", ["kea"], T.ct[:, 1536 + 512 * b:2048 + 512 * b], T.et[:, 3 - b:515 - b], ACT.Relu, bias=1.0, scale=-1.0)

    def weighted(label, deps, a, col):
        equal(label, deps, T.ct[:, a:a + 512], T.gw[:], T.et[:, 520:1032], F("g4"))()
        return lambda: act(label, [label, "kn"], T.ct[:, a:a + 512], T.ct[:, a:a + 512], ACT.Identity, scale=col)

    e_off = topo.engines(core, cs[peers[0]])
    e_on = [e for e in topo.engines(core, relay[r][0][0]) if e not in e_off]
    rid = [_dst(topo, c[0], core) for c in relay[r]]
    pid = [_dst(topo, cs[d], core) for d in peers]
    mine = L0 + NS * r
    c0 = mine - OWN * mk
    fl, sr = T.fl, T.sr

    for t in range(2):
        k = str(t)
        qx, x, xn = "qx" + k, T["x" + k], T["x%d" % (t + 1)]
        land, yq = "land" + k, "yq" + k

        def tr(c, b):
            mm("mt%d" % c, ["qx%d" % c, "uq"], b, qx, 128 * c, "uq", 0, 128)

        def sign(j, lo, hi, src, deps):
            act("sg", ["stc"] + deps, fl[:, 4 * lo + j:4 * hi:4], src, ACT.Sign, bias=T.stc[:, j:j + 1], scale=-1.0)

        def less(j, lo, hi, src, b, deps):
            ts("ls%d" % j, deps, fl[:, 4 * lo + j:4 * hi:4], src, bank[b][:, 15:16], ALU.is_lt)

        def layer(b, bk, deps, lo=0, hi=C):
            mm("mh%d" % b, ["Lw"] + deps, bk, "wq", 128 * b, qx, lo, hi)
            act("ht" if hi == C else "h0", ["mh%d" % b], T.ht[:, 8 + 4 * lo + b:8 + 4 * hi:4], bank[bk][:, 0:hi - lo], scale=0.03125)

        if t == 0:
            tr(0, 0)
            tr(1, 1)
            mm("ms0", ["upc", "ups", "qx2"], 3, "up", 0, qx, 0, C)
            tr(2, 2)
            mm("mth", ["uoc", "uos"], 4, "up", 128, qx, 0, C)
            mm("ms1", [], 5, "up", 0, qx, 0, C)
            mm("mp", [], 6, "uq", 0, qx, 0, C)
            act("stc", ["mt0"], T.stc[:, 0:1], bank[0][:, 15:16])
            less(1, 0, C, bank[3][:, 0:C], 1, ["ms0", "mt1"])
            less(2, 0, C, bank[3][:, 0:C], 2, ["mt2"])
            act("thr", ["mth"], T.thr[:], bank[4][:, 0:C])
            sign(0, 0, C, bank[5][:, 0:C], ["ms1"])
            act("sr", [], sr[:, 2:C + 2], bank[5][:, 0:C])
            gap()
            tt("pf", ["mp", "thr"], fl[:, 3:4 * C:4], bank[6][:, 0:C], T.thr[:], ALU.is_le)
            gap(2)
            layer(0, 7, ["stc"])
            layer(1, 0, [])
            kbk = (4, 5)
        else:
            for c in range(3):
                lo, hi = 128 * c, 128 * c + 128
                w("p", "stc")
                tr(c, 0)
                mm("ms0", ["sr", "sg"], 1, "up", 0, qx, lo, hi)
                mm("mth", ["thr"], 2, "up", 128, qx, lo, hi)
                if c < 2:
                    act("stc", ["mt%d" % c], T.stc[:, c:c + 1], bank[0][:, 15:16])
                else:
                    mm("mp1", ["h0"], 3, "uq", 0, qx, lo, hi)
                    tt("pf", ["mp", "thr"], fl[:, 3:4 * lo:4], bank[7][:, 0:lo], T.thr[:, 0:lo], ALU.is_le)
                    less(2, 0, lo, sr[:, 2:2 + lo], 0, ["sr", "mt2"])
                act("sr", ["ms0"], sr[:, 2 + lo:2 + hi], bank[1][:, 0:128])
                act("thr", ["mth"], T.thr[:, lo:hi], bank[2][:, 0:128])
                for j in range(min(c + 1, 2)):
                    sign(j, lo, hi, bank[1][:, 0:128], [])
                if c == 1:
                    sign(1, 0, lo, sr[:, 2:2 + lo], ["sr"])
                    mm("mp", [], 7, "uq", 0, qx, 0, hi)
                if c == 0:
                    for b in range(4):
                        layer(b, 3 + b, [], lo, hi)
            less(2, 256, C, sr[:, 258:C + 2], 0, ["sr"])
            tt("pf", ["mp1", "thr"], fl[:, 3 + 1024:4 * C:4], bank[3][:, 0:128], T.thr[:, 256:C], ALU.is_le)
            for b in range(4):
                layer(b, (4, 5, 6, 3)[b], ["pf"] if b == 3 else [], 128, C)
            kbk = (1, 2)
        quant("qfl", ["pf", "sg", "ls1", "ls2"], "qfl", 0, C, "fl", 0)
        if t:
            quant("qh", ["h0"], "qh", 0, 130, "ht", 0)
        for h in range(2):
            mm("mk%d" % h, ["qfl", "qhc", "sr"], kbk[h], "qhc", 128 * h, "qfl", 0, C)
        if t == 0:
            layer(2, 1, [])
            layer(3, 2, [])
            equal("kd", ["gd"], T.dm[:], T.sg[:, 0:NS], T.et[:, 520:520 + NS], p15)()
            act("gs", [], T.seg[:], T.sg[:, 0:NS], ACT.Sign)
            gap(5)
        for h, (a, b) in enumerate(((0, 24), (24, 56))):
            do("v", "sc%d" % h, ["mk%d" % h, "go"], V.tensor_tensor_scan, T.sc[:, C * h:C * h + C], T.z[:, 224:224 + C], bank[kbk[h]][:, 0:C], -STEP * 1024, ALU.add, ALU.max)
        for h, (a, b) in enumerate(((0, 24), (24, 56))):
            ts("ai", ["sc%d" % h, "kz"], T.ai[:, a:b], T.zm[:, a:b], T.sc[:, C * h + C - 1:C * h + C], ALU.mult, 16.0, ALU.add)
        if t == 0:
            quant("qy", ["ky"], "qc", 0, 128, "ct", 0)
        w("v", "ai", "g0")
        for b, ma in enumerate((480, 31)):
            ts("dg", [], T.dg[:, 56 * b:56 * b + 56], T.ai[:], ma, ALU.bitwise_and)
        gap()
        cp("dz", ["dg"], T.z[:, 0:224:4], T.dg[:, 0:56])
        ts("dz", [], T.z[:, 1:224:4], T.dg[:, 56:112], -16.0, ALU.add)
        gap()
        quant("qz", ["dz"], "qz", 0, 128, "z", 0)
        mm("mz", ["qz", "ht" if t else "qy"], 3, "qc", 0, "qz", 0, 128)
        quant("qh", ["ht"], "qh", 130 * t, C + 2, "ht", 520 * t)
        w("v", "mz")
        for q in range(4):
            src = bank[3][32 * q:32 * q + 32, q:48:4] if q < 3 else bank[3][96:128, 11:56:4]
            ts("ls", [], T.ls[32 * q:32 * q + 32, :], src, -1.0, ALU.mult, float(C + 1), ALU.add)
        so, stl = T["so" + k], T["stl" + k]
        picks("c", ["ls", "qh"], land, c0, c0 + NS, "qh", 0, C + 2, "ls", 0, 12)
        gap()
        tt("sa", ["ls", "sr", "kd", "g0", "gs"], T.sg[:, 0:NS], sr[:, 0:C + 2].indirect(T.ls[:, 0:12]), T.dm[:], ALU.mult)
        gap()
        do("v", "sb", ["sa"], V.tensor_tensor_scan, T.sg[:, NS:2 * NS], T.seg[:], T.sg[:, 0:NS], 0.0, ALU.mult, ALU.add)
        gap()
        cp("so", ["sb"], so[:], T.sg[:, NS + 15:2 * NS:16])
        pickc("c", ["qh"], land, c0, c0 + NS, "qh", 0, C + 2, "ls", 0, 12)
        cp("sown", [], stl[:, 12 * r + 4:12 * r + 7], T.sg[:, NS + 15 + OWN * mk:NS + OWN * mk + OWN:16])

        def piece(what, o, n):
            return so[:, 3 * o:3 * (o + n)] if what == "t" else u8(land, what, c0 + OWN * o, c0 + OWN * (o + n))

        def relayed(what, which):
            return [([rid[j]], e_on[4 * i:4 * i + 4], piece(what, relay[r][j][1], 2), T["rst" + k][:] if what == "t" else u8("rp" + k, what, 0, 2 * OWN))
                    for i, j in enumerate(which)]

        e = e_off
        send(["cs"], "ps" + k, [([rid[2 + i]], e[4 * i:4 * i + 4], piece("s", 2 * i, 2), u8("rp" + k, "s", 0, 2 * OWN)) for i in range(2)])
        send(["so"], "st" + k, relayed("t", (0, 1)) + [([pid[i]], (e[0:4], e[4:6], e[6:8])[i], piece("t", kk[d] // 2 * 2, 2), stl[:, 12 * r + 4 - 3 * (kk[d] % 2):12 * r + 10 - 3 * (kk[d] % 2)])
                                                      for i, d in enumerate(peers)])
        send(["cc"], "pc" + k, relayed("", (0, 1)))
        for which in ((0, 1), (2,)):
            send([], "pc" + k, [([pid[i]], (e[0:4], e[4:8], e)[i], piece("", kk[peers[i]], 1), u8(land, "", mine, mine + OWN)) for i in which])
        cnt["ps" + k], cnt["st" + k], cnt["pc" + k] = 4 * 7, 8 + 16, 16 + 16

        def offsets():
            mm("ml", ["qpr", "qwl"], 0, "qc", 128, "qpr", 0, 128)
            ts("off", ["ml"], T.off[:], bank[0][:, 0:96], F("ob"), ALU.add)

        if t == 0:
            iota("gw", T.gw[:], [[1, 32], [0, 4], [-1, 4]], 0, 0)
            quant("qpa", ["ga"], "qc", 896, 1024, "ct", 3584)
            unpackers(0, 1, 2, 3)
        mm("ma", ["qpa", "ht"], 6, "qc", 896, "qfl", 0, C)
        gap(6)
        ts("pr", ["ma"], T.pr[:, 0:C], bank[6][:, 0:C], 0.0, ALU.is_equal)
        gap(99)
        if t == 0:
            weigh = weighted("kw", ["gw", "kg"], 512, F("w3"))
            quant("qe", ["kes"], "qc", 384, 896, "ct", 1536)
            quant("qpr", ["pr", "gc"], "qpr", 0, 128, "pr", 0)
        else:
            weighted("kv", ["gv"], 1024, F("wl"))()
            quant("qpr", ["pr"], "qpr", 0, 128, "pr", 0)
            cp("pw", [], fl[:, 3:4 * C:4], T.pr[:, 0:C])
            offsets()
            quant("qpw", ["pw"], "qfl", 0, C, "fl", 0)
        wn = T.wn
        w("v", "st" + k, "sown", "kc")
        for c in range(3):
            do("v", "w1", [], V.tensor_tensor_scan, wn[:, 8 * c:8 * c + 8], stl[:, 4 + c:96:12], stl[:, 4 + c:96:12], -1e29, ALU.max, ALU.max)
            act("w2%d" % c, ["w1"], wn[:, 24 + 8 * c:32 + 8 * c], wn[:, 8 * c:8 * c + 8], ACT.Sign, bias=wn[:, 8 * c + 7:8 * c + 8], scale=-1.0,
                accum_out=wn[:, 56 + c:57 + c])
        for c in range(3):
            ts("tl", ["w2%d" % c], T.tl[:, c:c + 1], wn[:, 56 + c:57 + c], float(NS), ALU.mult, wn[:, 60 + c:61 + c], ALU.add)
        a = OWN * mk
        pickc("t", ["tl", "cc", "pc" + k], yq, a, a + OWN, land, L0, LAND, "tl", 0, 3)
        picks("t", ["tl", "cs", "ps" + k], yq, a, a + OWN, land, L0, LAND, "tl", 0, 3)
        for what, sm, lb in (("", "yc", "tc"), ("s", "ys", "ts"))[::1 - 2 * t]:
            send([lb], sm + k, [(pid, e_off, u8(yq, what, a, a + OWN), u8(yq, what, a, a + OWN))])
            cnt[sm + k] = 3 * len(e_off)
        if t == 0:
            weigh()
            quant("qwl", ["kw"], "qc", 128, 256, "ct", 512)
            offsets()
            quant("vq", ["Lv"], "vq", 0, 128, "vt", 0)
            iota("gv", T.gw[:], [[1, 512]], -3, 0)
        else:
            quant("qww", ["kv"], "qc", 256, 384, "ct", 1024)
            mm("mw", ["qpw", "qww", "ls"], 3, "qc", 256, "qfl", 0, C)
            act("wlb", ["mw"], T.wlb[0:8, :], bank[3][0:8, 0:C], ACT.Identity, bias=fc[0:8, cols["pw"]:cols["pw"] + 1], scale=0.25)
            dma("q", "so_", ["wlb"], T.wl[:], T.wlb[0:8, :])
        for b, bk in enumerate((1, 2, 4, 5)):
            mm("md%d" % b, ["qe", "tc", "ts", "yc" + k, "ys" + k], bk, "qc", 384 + 128 * b, yq, 0, NS)
            yo = T.yt[:, 4 + b:4 + 4 * NS:4]
            if b % 2 == 0:
                act("ya", ["md%d" % b], yo, bank[bk][:, 0:NS])
            else:
                cp("yv", ["md%d" % b], yo, bank[bk][:, 0:NS])

        def add(lb, a, b):
            tt(lb, ["yv", "ya", "off"], xn[:, 16 * a:16 * b], T.yt[:, 0:4 * NS + 4].indirect(T.off[:, a:b]), x[:, 16 * a:16 * b], ALU.add)

        add("xn0", 0, 32)
        for c in range(3):
            if c < 2:
                add("xn%d" % (c + 1), 32 * c + 32, 32 * c + 40)
            quant("qx%d" % c, ["xn%d" % c], "qx%d" % (t + 1), 128 * c, 128 * c + 128, "x%d" % (t + 1), 512 * c)
            if c < 2:
                add("xn%d" % (c + 1), 32 * c + 40, 32 * c + 64)

    for c in range(3):
        a, b = 128 * c, 128 * c + 128
        mm("my%d" % c, ["qx%d" % c, "vq"], 5 + c, "vq", 0, "qx2", a, b)
        if c < 2:
            act("yo%d" % c, ["my%d" % c], T.yo[:, a:b], bank[5 + c][:, 0:128])
        else:
            cp("yo%d" % c, ["my%d" % c], T.yo[:, a:b], bank[5 + c][:, 0:128])
        dma("q", "so_", ["qx%d" % c], T.oc[:, 4 * a:4 * b], T.qx2[:, a:b].bitcast(dt.uint8))
        dma("q", "so_", ["yo%d" % c], T.y[:, a:b], T.yo[:, a:b])
    for i in range(4):
        dma("s", "ss", ["qx0", "qx1", "qx2"], T.osc[4 * i:4 * i + 4, :], T.qx2s[32 * i:32 * i + 4, :])
    w("s", "ss")
    for lb in list(cnt):
        if done.get(lb, 0) < cnt[lb]:
            w("g" if lb == "lr" else "q", lb)
